import numpy as np
import ml_dtypes


def mxq(x, axis, fmt="e4m3"):
    dtype, down = {"e4m3": (ml_dtypes.float8_e4m3fn, 7), "e5m2": (ml_dtypes.float8_e5m2, 14)}[fmt]
    v = np.moveaxis(np.asarray(x, np.float32).astype(ml_dtypes.bfloat16).astype(np.float64), axis, -1)
    blocks = v.reshape(v.shape[:-1] + (-1, 32))
    amax = np.abs(blocks).max(-1, keepdims=True)
    byte = np.maximum(np.where(amax > 0, np.frexp(amax)[1] - 1 + 127, 0) - down, 1)
    scale = np.exp2(byte - 127.0)
    codes = (blocks / scale).astype(np.float32).astype(dtype).astype(np.float64)
    return np.moveaxis((codes * scale).reshape(v.shape), -1, axis)


WIDE = False


def mx_kscale(k):
    if not WIDE:
        return np.ones(k)
    levels = np.array([10, -10, 5, -5, 0])
    if k % 512:
        return np.exp2(np.random.permutation(np.resize(levels, k // 32))).repeat(32)
    a = np.empty((k // 512, 16))
    for p in range(k // 512):
        a[p, :8] = np.random.permutation(np.resize(levels, 8))
        for g in range(8):
            far = levels[np.abs(levels - a[p, g]) >= 10]
            a[p, g + 8] = far[np.random.randint(len(far))]
    return np.exp2(a.ravel()).repeat(32)


BF16 = ml_dtypes.bfloat16


def bf(x):
    return np.asarray(x, np.float32).astype(BF16)


def f64(x):
    return np.asarray(x).astype(np.float64)


M, N, K = 1024, 1024, 512


def poisson_residual(u, v, y):
    theta = mxq(u, 1, "e4m3") @ mxq(v, 1, "e4m3").T
    return y - np.exp(theta)


def draw0():
    s, t, p = mx_kscale(K), mx_kscale(N), mx_kscale(M)
    return {"u": bf(np.random.standard_normal((M, K)) * s[None, :]),
            "v": bf(np.random.standard_normal((N, K)) * 0.5 / np.sqrt(K) / s[None, :]),
            "y": bf(np.random.uniform(0.0, 2.5, (M, N))),
            "gm": bf((1.0 + 0.1 * np.random.standard_normal(M)) * p),
            "gn": bf((1.0 + 0.1 * np.random.standard_normal(N)) * t),
            "us": bf(np.random.standard_normal((M, K)) / np.sqrt(M) / p[:, None]),
            "vs": bf(np.random.standard_normal((N, K)) / np.sqrt(N) / t[:, None])}


def core(u, v, y, gm, gn, us, vs):
    r = poisson_residual(f64(u), f64(v), f64(y))
    rn = r * f64(gn)[None, :]
    gu = mxq(rn, 1, "e4m3") @ mxq(f64(vs), 0, "e4m3")
    rm = r * f64(gm)[:, None]
    gv = mxq(rm, 0, "e4m3").T @ mxq(f64(us), 0, "e4m3")
    return gu, gv


def e4m3fn_bytes(y):
    return np.clip(np.asarray(y, np.float64), -448.0, 448.0).astype(np.float32).astype(ml_dtypes.float8_e4m3fn).view(np.uint8)


def e4m3fn_values(b):
    return np.asarray(b, np.uint8).view(ml_dtypes.float8_e4m3fn).astype(np.float64)


def setup_inputs():
    d = draw0()
    x0 = np.asarray(d['vs']).astype(np.float64)
    s = (np.max(np.abs(x0), axis=(1,), keepdims=True) / 448.0).astype(np.float32)
    out = {}
    for k, v in d.items():
        if k == 'vs':
            out['vs_bytes'] = e4m3fn_bytes(x0 / s.astype(np.float64))
            out['vs_scale'] = s
        else:
            out[k] = v
    return out


def reference(u, v, y, gm, gn, us, vs_bytes, vs_scale):
    return core(u, v, y, gm, gn, us, e4m3fn_values(vs_bytes) * vs_scale.astype(np.float64))

@@ -1,0 +1,332 @@
+from contextlib import ExitStack
+
+import concourse.mybir as mybir
+from concourse.masks import make_identity
+
+M, N, K = 1024, 1024, 512
+FLOPS = 3 * 2 * M * N * K
+
+F32 = mybir.dt.float32
+BF16 = mybir.dt.bfloat16
+U32 = mybir.dt.uint32
+U8 = mybir.dt.uint8
+FP8 = mybir.dt.float8_e4m3fn
+FP8X4 = mybir.dt.float8_e4m3fn_x4
+MULT = mybir.AluOpType.mult
+ADD = mybir.AluOpType.add
+EXP = mybir.ActivationFunctionType.Exp
+COPY = mybir.ActivationFunctionType.Copy
+
+P = 128
+PACK = 4
+PASS = P * PACK
+ROW_OF_SLOT = (0, 2, 1, 3)
+
+
+def tile_weightedpoissonresidualproducts_kernel(tc, u, v, y, gm, gn, us, vs_bytes, vs_scale, out_0, out_1):
+    nc = tc.nc
+    with ExitStack() as ctx:
+        sb = ctx.enter_context(tc.tile_pool(name="sb", bufs=1))
+        ps = ctx.enter_context(tc.psum_pool(name="ps", bufs=1))
+        ctx.enter_context(tc.manual_schedule())
+        T = {}
+
+        def new(key, shape, dtype, tag="", bufs=1):
+            T[key] = sb.tile(shape, dtype, name=key, tag=tag or key, bufs=bufs, align_bytes=256)
+            return T[key]
+
+        def bank(key, tag, shape):
+            T[key] = ps.tile(shape, F32, name=key, tag=tag, bufs=BANKS[tag])
+            return T[key]
+
+        def operand(key, width):
+            new(key + "_codes", [P, width], U32)
+            new(key + "_scales", [P, width], U8)
+
+        def quantize(key, cols, values):
+            nc.vector.quantize_mx(out=T[key + "_codes"][:, cols].bitcast(FP8X4), scales=T[key + "_scales"][:, cols], in_=values)
+
+        def product(out, lhs, cols, rhs, start, stop):
+            nc.tensor.matmul_mx(
+                out=out,
+                lhsT=T[lhs + "_codes"][:, cols].bitcast(FP8X4),
+                lhsT_scale=T[lhs + "_scales"][:, cols],
+                rhs=T[rhs + "_codes"][:].bitcast(FP8X4),
+                rhs_scale=T[rhs + "_scales"][:],
+                start=start,
+                stop=stop,
+            )
+
+        for i in range(2):
+            operand("u%d" % i, PASS)
+            operand("us%d" % i, K)
+            operand("vs%d" % i, K)
+        for i in range(4):
+            operand("v%d" % i, 2 * P)
+            operand("rn%d" % i, PASS)
+            new("rn_rows%d" % i, [P, PACK, 2, 2 * P], BF16)
+        for i in range(16):
+            operand("rm%d" % i, P)
+        new("gn_neg", [P, 8, 2, 64], BF16)
+
+        def constants():
+            ident = new("ident", [P, P], F32)
+            make_identity(nc, ident[:])
+            nc.vector.memset(new("gn_row", [P, N], BF16)[:], 0.0)
+            nc.vector.memset(new("minus_ones", [P, P], BF16)[:], -1.0)
+
+        def negate_identity():
+            nc.vector.tensor_scalar(out=new("neg_ident", [P, P], BF16)[:], in0=T["ident"][:], scalar1=-1.0, scalar2=None, op0=MULT)
+
+        def load_u(g, a):
+            src = u.rearrange("(g p t) k -> g p t k", p=P, t=PACK)[g]
+            nc.sync.dma_start(out=new("u_raw%d%d" % (g, a), [P, 2, K], BF16)[:], in_=src[:, 2 * a : 2 * a + 2, :])
+
+        def load_v(c):
+            nc.sync.dma_start(out=new("v_raw%d" % c, [P, 2, K], BF16)[:], in_=v.rearrange("(c p r) k -> c p r k", p=P, r=2)[c])
+
+        def load_y(q):
+            src = y.rearrange("(g p t) n -> g p t n", p=P, t=PACK)[q // 2]
+            nc.sync.dma_start(out=new("y%d" % q, [P, PACK, PASS], BF16)[:], in_=src[:, :, PASS * (q % 2) : PASS * (q % 2 + 1)])
+
+        def load_us(g):
+            nc.sync.dma_start(out=new("us_raw%d" % g, [P, PACK, K], BF16)[:], in_=us.rearrange("(g p t) k -> g p t k", p=P, t=PACK)[g])
+
+        def load_vs(h):
+            nc.sync.dma_start(out=new("vs_raw%d" % h, [P, PACK, K], U8)[:], in_=vs_bytes.rearrange("(h p t) k -> h p t k", p=P, t=PACK)[h])
+
+        def load_gn():
+            nc.sync.dma_start(out=T["gn_row"][0:1, :], in_=gn.rearrange("(o n) -> o n", o=1))
+
+        def load_gm():
+            nc.sync.dma_start(out=new("gm_raw", [P, 2, PACK], BF16)[:], in_=gm.rearrange("(g p t) -> p g t", p=P, t=PACK))
+
+        def load_vs_scale():
+            nc.sync.dma_start(out=new("vs_sc", [P, 2, PACK], F32)[:], in_=vs_scale.rearrange("(h p t) o -> p h (t o)", p=P, t=PACK))
+
+        def negate_gm():
+            nc.vector.tensor_scalar(out=new("gm_neg", [P, 2, PACK], F32)[:], in0=T["gm_raw"][:], scalar1=-1.0, scalar2=None, op0=MULT)
+
+        def spread_gn(h, tag):
+            b = bank("gn_ps%d" % h, tag, [P, PASS])
+            nc.tensor.matmul(out=b[:], lhsT=T["minus_ones"][:], rhs=T["gn_row"][:, PASS * h : PASS * (h + 1)], start=True, stop=True)
+
+        def copy_gn(h):
+            nc.scalar.copy(out=T["gn_neg"][:, 4 * h : 4 * h + 4, :, :], in_=T["gn_ps%d" % h][:].rearrange("p (j i w) -> p j w i", j=4, w=2))
+
+        def turn_k(name, tag):
+            b = bank(name + "_ps", tag, [P, 2, 2, P])
+            for r in range(2):
+                words = T[name][:, r, :].bitcast(F32)
+                for w in range(2):
+                    nc.tensor.transpose(b[:, r, w, :], words[:, w : 2 * P : 2], T["ident"][:])
+
+        def turn_rn(q, a, tag):
+            b = bank("rn_t%d%d_ps" % (q, a), tag, [P, 2, 2, P])
+            for r in range(2):
+                for w in range(2):
+                    nc.tensor.transpose(b[:, r, w, :], T["rn_rows%d" % q][:, 2 * a + r, w, :].bitcast(F32), T["ident"][:])
+
+        def copy_words(name, order, engine):
+            dst = new(name + "_words", [P, PASS], F32, "words", 6)
+            src = T[name + "_ps"][:].rearrange("p r w m -> p " + order)
+            view = dst[:].rearrange("p (%s) -> p %s" % (order, order), r=2, w=2)
+            if engine == "s":
+                nc.scalar.copy(out=view, in_=src)
+            else:
+                nc.vector.tensor_copy(out=view, in_=src)
+
+        def copy_u(g, a, engine):
+            copy_words("u_raw%d%d" % (g, a), "r m w", engine)
+
+        def copy_v(c, engine):
+            copy_words("v_raw%d" % c, "m r w", engine)
+
+        def copy_rn(q, a, engine):
+            copy_words("rn_t%d%d" % (q, a), "r m w", engine)
+
+        def quant_u(g, a):
+            quantize("u%d" % g, slice(2 * P * a, 2 * P * (a + 1)), T["u_raw%d%d_words" % (g, a)][:].bitcast(BF16))
+
+        def quant_v(c):
+            quantize("v%d" % c, slice(0, 2 * P), T["v_raw%d_words" % c][:].bitcast(BF16))
+
+        def quant_rn(q, a):
+            quantize("rn%d" % q, slice(2 * P * a, 2 * P * (a + 1)), T["rn_t%d%d_words" % (q, a)][:].bitcast(BF16))
+
+        def widen_vs(h, slot, engine):
+            if slot == 0:
+                new("vs_wide%d" % h, [P, PACK, K], BF16)
+            t = ROW_OF_SLOT[slot]
+            codes = T["vs_raw%d" % h][:, t, :].bitcast(FP8)
+            scale = T["vs_sc"][:, h, t : t + 1]
+            if engine == "s":
+                nc.scalar.activation(out=T["vs_wide%d" % h][:, slot, :], in_=codes, func=COPY, scale=scale)
+            else:
+                nc.vector.tensor_scalar(out=T["vs_wide%d" % h][:, slot, :], in0=codes, scalar1=scale, scalar2=None, op0=MULT)
+
+        def weave(name, part, engine, parts=2):
+            if part == 0:
+                new(name + "_woven", [P, K, PACK], BF16)
+            cols = slice(part * K // parts, (part + 1) * K // parts)
+            if engine == "g":
+                nc.gpsimd.tensor_scalar(
+                    out=T[name + "_woven"][:, cols, :], in0=T[name][:, :, cols].rearrange("p t c -> p c t"),
+                    scalar1=1.0, scalar2=0.0, op0=MULT, op1=ADD,
+                )
+                return
+            dst = T[name + "_woven"][:, cols, :].rearrange("p (c i) t -> p c t i", i=4)
+            src = T[name][:, :, cols].rearrange("p t (c i) -> p c t i", i=4)
+            if engine == "s":
+                nc.scalar.copy(out=dst, in_=src)
+            else:
+                nc.vector.tensor_copy(out=dst, in_=src)
+
+        def quant_woven(key, name):
+            quantize(key, slice(0, K), T[name + "_woven"][:].rearrange("p c t -> p (c t)"))
+
+        def theta(s, tag):
+            j = s % 8
+            b = bank("theta%d" % s, tag, [P, PASS])
+            product(b[:], "v%d" % (j // 2), slice(P * (j % 2), P * (j % 2 + 1)), "u%d" % (s // 8), True, True)
+
+        def rate(s):
+            nc.scalar.activation(out=new("rate%d" % s, [P, PASS], F32, "rate", 10)[:], in_=T["theta%d" % s][:], func=EXP)
+
+        def open_residual(s, tag):
+            b = bank("res%d" % s, tag, [P, PACK, P])
+            cols = slice(P * (s % 4), P * (s % 4 + 1))
+            nc.tensor.matmul(out=b[:], lhsT=T["neg_ident"][:], rhs=T["y%d" % (s // 4)][:, :, cols], start=True, stop=False)
+
+        def add_rate(s, t):
+            nc.tensor.matmul(
+                out=T["res%d" % s][:, t, :], lhsT=T["rate%d" % s][:, P * t : P * (t + 1)], rhs=T["ident"][:],
+                is_transpose=True, start=False, stop=(t == PACK - 1),
+            )
+
+        def close_residual(s):
+            for t in range(PACK):
+                add_rate(s, t)
+
+        def residual(s, tag):
+            b = bank("res%d" % s, tag, [P, PACK, P])
+            cols = slice(P * (s % 4), P * (s % 4 + 1))
+            for t in range(PACK + 1):
+                if t < PACK:
+                    nc.tensor.matmul(out=b[:, t, :], lhsT=T["neg_ident"][:], rhs=T["y%d" % (s // 4)][:, t, cols], start=(t == 0), stop=False)
+                if t > 0:
+                    add_rate(s, t - 1)
+
+        def weigh_m(s):
+            g = s // 8
+            nc.vector.tensor_tensor(
+                out=new("rm_woven%d" % s, [P, P, PACK], BF16, "rm_woven", 4)[:],
+                in0=T["res%d" % s][:].rearrange("p t n -> p n t"),
+                in1=T["gm_neg"][:, g : g + 1, :].to_broadcast([P, P, PACK]),
+                op=MULT,
+            )
+
+        def weigh_n(s):
+            j = s % 8
+            nc.vector.tensor_tensor(
+                out=T["rn_rows%d" % (s // 4)][:, :, :, 64 * (s % 4) : 64 * (s % 4 + 1)],
+                in0=T["res%d" % s][:].rearrange("p t (i w) -> p t w i", w=2),
+                in1=T["gn_neg"][:, j : j + 1, :, :].to_broadcast([P, PACK, 2, 64]),
+                op=MULT,
+            )
+
+        def quant_rm(s):
+            quantize("rm%d" % s, slice(0, P), T["rm_woven%d" % s][:].rearrange("p n t -> p (n t)"))
+
+        def gu_pass(g, t, h, tag):
+            if h == 0:
+                bank("gu%d%d" % (g, t), tag, [P, K])
+            product(T["gu%d%d" % (g, t)][:], "rn%d" % (2 * g + h), slice(P * t, P * (t + 1)), "vs%d" % h, h == 0, h == 1)
+
+        def gv_pass(j, g, tag):
+            if g == 0:
+                bank("gv%d" % j, tag, [P, K])
+            product(T["gv%d" % j][:], "rm%d" % (8 * g + j), slice(0, P), "us%d" % g, g == 0, g == 1)
+
+        def store(name, dst, engine):
+            res = new(name + "_out", [P, K], F32, "result", 10)
+            if engine == "s":
+                nc.scalar.copy(out=res[:], in_=T[name][:])
+            else:
+                nc.vector.tensor_copy(out=res[:], in_=T[name][:])
+            nc.sync.dma_start(out=dst, in_=res[:])
+
+        def store_gu(g, t, engine):
+            store("gu%d%d" % (g, t), out_0.rearrange("(g p t) k -> g t p k", p=P, t=PACK)[g, t], engine)
+
+        def store_gv(j, engine):
+            store("gv%d" % j, out_1[P * j : P * (j + 1), :], engine)
+
+
+        BANKS = {"m": 4, "r": 4}
+        constants()
+        load_u(0, 0); load_u(0, 1); load_v(0); load_vs_scale(); load_vs(0); load_gn(); load_v(1); load_y(0); load_gm()
+        load_v(2); load_v(3); load_vs(1); load_u(1, 0); load_u(1, 1); load_y(1); load_us(0); load_us(1); load_y(2); load_y(3)
+        negate_identity()
+        turn_k("u_raw00", "m"); copy_u(0, 0, "s")
+        turn_k("u_raw01", "m"); copy_u(0, 1, "s")
+        turn_k("v_raw0", "m"); copy_v(0, "s")
+        widen_vs(0, 0, "v")
+        quant_u(0, 0); widen_vs(0, 1, "v"); quant_u(0, 1); widen_vs(0, 2, "v")
+        quant_v(0)
+        spread_gn(0, "r"); spread_gn(1, "r")
+        turn_k("v_raw1", "m"); copy_gn(0); copy_v(1, "v")
+        theta(0, "m"); theta(1, "m")
+        open_residual(0, "r"); open_residual(1, "r")
+        rate(0); rate(1); copy_gn(1)
+        widen_vs(0, 3, "v")
+        quant_v(1)
+        weave("vs_wide0", 0, "v"); weave("vs_wide0", 1, "v")
+        negate_gm()
+        turn_k("v_raw2", "m"); close_residual(0); close_residual(1); copy_v(2, "s")
+        theta(2, "m"); theta(3, "m"); rate(2); rate(3)
+        turn_k("v_raw3", "m"); copy_v(3, "s"); residual(2, "r"); residual(3, "r"); turn_k("u_raw10", "m"); copy_u(1, 0, "s")
+        weigh_m(0); weigh_n(0); quant_woven("vs0", "vs_wide0"); quant_rm(0); quant_v(2)
+        theta(4, "m"); theta(5, "m"); rate(4); rate(5)
+        weigh_m(1); weigh_n(1); quant_v(3); quant_rm(1); quant_u(1, 0)
+        turn_k("u_raw11", "m"); copy_u(1, 1, "s"); residual(4, "r"); residual(5, "r")
+        theta(6, "m"); theta(7, "m"); widen_vs(1, 0, "s"); widen_vs(1, 1, "s"); rate(6); rate(7)
+        weigh_m(2); weigh_n(2); quant_u(1, 1); quant_rm(2)
+        theta(8, "m"); theta(9, "m"); widen_vs(1, 2, "s"); widen_vs(1, 3, "s"); rate(8); rate(9)
+        weigh_n(3); weigh_m(3)
+        residual(6, "r"); residual(7, "r"); turn_rn(0, 0, "m"); copy_rn(0, 0, "s"); turn_rn(0, 1, "m"); copy_rn(0, 1, "s")
+        theta(10, "m"); theta(11, "m"); rate(10); rate(11)
+        weigh_m(4); quant_rm(3); weigh_n(4); quant_rm(4)
+        weigh_n(5); weave("vs_wide1", 0, "v"); weigh_n(6); weave("vs_wide1", 1, "v"); weigh_n(7); quant_rn(0, 0); quant_rn(0, 1); weigh_m(5)
+        weave("us_raw0", 0, "s", 4); weave("us_raw0", 1, "s", 4)
+        residual(8, "r"); turn_rn(1, 0, "m"); copy_rn(1, 0, "s"); turn_rn(1, 1, "m"); copy_rn(1, 1, "s")
+        weave("us_raw0", 2, "s", 4); weave("us_raw0", 3, "s", 4)
+        quant_woven("vs1", "vs_wide1"); quant_rm(5); weigh_m(6); weigh_m(7); quant_rn(1, 0); quant_rm(6); quant_rn(1, 1); quant_rm(7)
+        residual(9, "r"); residual(10, "r"); residual(11, "r")
+        weave("us_raw1", 0, "s", 4); weave("us_raw1", 1, "s", 4)
+        for t in (0, 1):
+            gu_pass(0, t, 0, "m"); gu_pass(0, t, 1, "m"); store_gu(0, t, "s")
+        theta(12, "m"); theta(13, "m"); rate(12); rate(13)
+        for t in (2, 3):
+            gu_pass(0, t, 0, "m"); gu_pass(0, t, 1, "m"); store_gu(0, t, "s")
+        theta(14, "m"); theta(15, "m"); rate(14); rate(15)
+        weigh_m(8); weave("us_raw1", 1, "v", 2); weigh_n(8); quant_woven("us0", "us_raw0"); quant_rm(8); quant_woven("us1", "us_raw1")
+        weigh_m(9); weigh_n(9)
+        residual(12, "r")
+        weigh_m(10); quant_rm(9); weigh_n(10); quant_rm(10); weigh_n(11); weigh_m(11)
+        for j in (0, 1):
+            gv_pass(j, 0, "m"); gv_pass(j, 1, "m"); store_gv(j, "s")
+        residual(13, "r"); residual(14, "r"); turn_rn(2, 0, "m"); copy_rn(2, 0, "s"); turn_rn(2, 1, "m"); copy_rn(2, 1, "s"); residual(15, "r")
+        weigh_m(12); quant_rm(11); weigh_n(12); quant_rm(12)
+        for j in (2, 3, 4):
+            gv_pass(j, 0, "m"); gv_pass(j, 1, "m"); store_gv(j, "s")
+        weigh_n(13); weigh_n(14); weigh_n(15); quant_rn(2, 0); quant_rn(2, 1); weigh_m(13)
+        turn_rn(3, 0, "m"); copy_rn(3, 0, "s"); turn_rn(3, 1, "m"); copy_rn(3, 1, "s")
+        gu_pass(1, 0, 0, "r"); gu_pass(1, 1, 0, "m")
+        weigh_m(14); quant_rm(13); quant_rn(3, 0); weigh_m(15); quant_rm(14); quant_rn(3, 1); quant_rm(15)
+        gv_pass(5, 0, "m"); gv_pass(5, 1, ""); store_gv(5, "s"); gu_pass(1, 0, 1, ""); gu_pass(1, 1, 1, ""); store_gu(1, 0, "s")
+        gv_pass(6, 0, "r"); gv_pass(6, 1, "")
+        store_gu(1, 1, "v"); store_gv(6, "s")
+        gu_pass(1, 2, 0, "m"); gu_pass(1, 2, 1, ""); store_gu(1, 2, "v")
+        gu_pass(1, 3, 0, "m"); gu_pass(1, 3, 1, ""); store_gu(1, 3, "s")
+        gv_pass(7, 0, "r"); gv_pass(7, 1, ""); store_gv(7, "v")

@@ -17,10 +17,15 @@ ADD = mybir.AluOpType.add
 EXP = mybir.ActivationFunctionType.Exp
 COPY = mybir.ActivationFunctionType.Copy
 
+ENG = mybir.EngineType
+PINNED = {ENG.PE, ENG.SP, ENG.Pool, ENG.DVE, ENG.Activation}
+
 P = 128
 PACK = 4
 PASS = P * PACK
 ROW_OF_SLOT = (0, 2, 1, 3)
+PIECE = 384
+WOVEN_BY_GPSIMD = (("us_raw0", "us0"), ("us_raw1", "us1"), ("vs_wide1", "vs1"))
 
 
 def tile_weightedpoissonresidualproducts_kernel(tc, u, v, y, gm, gn, us, vs_bytes, vs_scale, out_0, out_1):
@@ -28,7 +33,7 @@ def tile_weightedpoissonresidualproducts_kernel(tc, u, v, y, gm, gn, us, vs_byte
     with ExitStack() as ctx:
         sb = ctx.enter_context(tc.tile_pool(name="sb", bufs=1))
         ps = ctx.enter_context(tc.psum_pool(name="ps", bufs=1))
-        ctx.enter_context(tc.manual_schedule())
+        ctx.enter_context(tc.manual_schedule(engines=PINNED))
         T = {}
 
         def new(key, shape, dtype, tag="", bufs=1):
@@ -46,13 +51,13 @@ def tile_weightedpoissonresidualproducts_kernel(tc, u, v, y, gm, gn, us, vs_byte
         def quantize(key, cols, values):
             nc.vector.quantize_mx(out=T[key + "_codes"][:, cols].bitcast(FP8X4), scales=T[key + "_scales"][:, cols], in_=values)
 
-        def product(out, lhs, cols, rhs, start, stop):
+        def product(out, lhs, cols, rhs, start, stop, moving=slice(0, PASS)):
             nc.tensor.matmul_mx(
                 out=out,
                 lhsT=T[lhs + "_codes"][:, cols].bitcast(FP8X4),
                 lhsT_scale=T[lhs + "_scales"][:, cols],
-                rhs=T[rhs + "_codes"][:].bitcast(FP8X4),
-                rhs_scale=T[rhs + "_scales"][:],
+                rhs=T[rhs + "_codes"][:, moving].bitcast(FP8X4),
+                rhs_scale=T[rhs + "_scales"][:, moving],
                 start=start,
                 stop=stop,
             )
@@ -65,8 +70,8 @@ def tile_weightedpoissonresidualproducts_kernel(tc, u, v, y, gm, gn, us, vs_byte
             operand("v%d" % i, 2 * P)
             operand("rn%d" % i, PASS)
             new("rn_rows%d" % i, [P, PACK, 2, 2 * P], BF16)
-        for i in range(16):
-            operand("rm%d" % i, P)
+        for i in range(8):
+            operand("rm%d" % i, 2 * P)
         new("gn_neg", [P, 8, 2, 64], BF16)
 
         def constants():
@@ -96,13 +101,13 @@ def tile_weightedpoissonresidualproducts_kernel(tc, u, v, y, gm, gn, us, vs_byte
             nc.sync.dma_start(out=new("vs_raw%d" % h, [P, PACK, K], U8)[:], in_=vs_bytes.rearrange("(h p t) k -> h p t k", p=P, t=PACK)[h])
 
         def load_gn():
-            nc.sync.dma_start(out=T["gn_row"][0:1, :], in_=gn.rearrange("(o n) -> o n", o=1))
+            nc.scalar.dma_start(out=T["gn_row"][0:1, :], in_=gn.rearrange("(o n) -> o n", o=1))
 
         def load_gm():
-            nc.sync.dma_start(out=new("gm_raw", [P, 2, PACK], BF16)[:], in_=gm.rearrange("(g p t) -> p g t", p=P, t=PACK))
+            nc.scalar.dma_start(out=new("gm_raw", [P, 2, PACK], BF16)[:], in_=gm.rearrange("(g p t) -> p g t", p=P, t=PACK))
 
         def load_vs_scale():
-            nc.sync.dma_start(out=new("vs_sc", [P, 2, PACK], F32)[:], in_=vs_scale.rearrange("(h p t) o -> p h (t o)", p=P, t=PACK))
+            nc.scalar.dma_start(out=new("vs_sc", [P, 2, PACK], F32)[:], in_=vs_scale.rearrange("(h p t) o -> p h (t o)", p=P, t=PACK))
 
         def negate_gm():
             nc.vector.tensor_scalar(out=new("gm_neg", [P, 2, PACK], F32)[:], in0=T["gm_raw"][:], scalar1=-1.0, scalar2=None, op0=MULT)
@@ -190,6 +195,59 @@ def tile_weightedpoissonresidualproducts_kernel(tc, u, v, y, gm, gn, us, vs_byte
             b = bank("theta%d" % s, tag, [P, PASS])
             product(b[:], "v%d" % (j // 2), slice(P * (j % 2), P * (j % 2 + 1)), "u%d" % (s // 8), True, True)
 
+        def load_v_single(j):
+            nc.sync.dma_start(out=new("v_one%d" % j, [P, K], BF16)[:], in_=v[P * j : P * (j + 1), :])
+
+        def turn_v_single(j, tag):
+            b = bank("v_one%d_ps" % j, tag, [P, 2, P])
+            words = T["v_one%d" % j][:].bitcast(F32)
+            for w in range(2):
+                nc.tensor.transpose(b[:, w, :], words[:, w : 2 * P : 2], T["ident"][:])
+
+        def copy_v_single(j, engine):
+            dst = new("v_one%d_words" % j, [P, P, 2], F32)
+            src = T["v_one%d_ps" % j][:].rearrange("p w m -> p m w")
+            if engine == "s":
+                nc.scalar.copy(out=dst[:], in_=src)
+            else:
+                nc.vector.tensor_copy(out=dst[:], in_=src)
+
+        def quant_v_single(j):
+            quantize("v0", slice(P * j, P * (j + 1)), T["v_one%d_words" % j][:].rearrange("p m w -> p (m w)").bitcast(BF16))
+
+        def theta_half(a, tag):
+            b = bank("theta_half%d" % a, tag, [P, 2 * P])
+            product(b[:], "v0", slice(0, P), "u0", True, True, slice(2 * P * a, 2 * P * (a + 1)))
+
+        def rate_half(a):
+            if a == 0:
+                new("rate0", [P, PASS], F32, "rate", 10)
+            nc.scalar.activation(out=T["rate0"][:, 2 * P * a : 2 * P * (a + 1)], in_=T["theta_half%d" % a][:], func=EXP)
+
+        def close_half(a):
+            add_rate(0, 2 * a)
+            add_rate(0, 2 * a + 1)
+
+        def piece_parts(k):
+            parts = []
+            for i, (name, key) in enumerate(WOVEN_BY_GPSIMD):
+                lo, hi = max(PIECE * k, K * i), min(PIECE * (k + 1), K * (i + 1))
+                if lo < hi:
+                    parts.append((name, key, slice(lo - K * i, hi - K * i), slice(lo - PIECE * k, hi - PIECE * k)))
+            return parts
+
+        def weave_piece(k):
+            dst = new("piece%d" % k, [P, PIECE, PACK], BF16, "vs_wide0_woven", 1)
+            for name, key, cols, place in piece_parts(k):
+                nc.gpsimd.tensor_scalar(
+                    out=dst[:, place, :], in0=T[name][:, :, cols].rearrange("p t c -> p c t"),
+                    scalar1=1.0, scalar2=0.0, op0=MULT, op1=ADD,
+                )
+
+        def quant_piece(k):
+            for name, key, cols, place in piece_parts(k):
+                quantize(key, cols, T["piece%d" % k][:, place, :].rearrange("p c t -> p (c t)"))
+
         def rate(s):
             nc.scalar.activation(out=new("rate%d" % s, [P, PASS], F32, "rate", 10)[:], in_=T["theta%d" % s][:], func=EXP)
 
@@ -219,8 +277,10 @@ def tile_weightedpoissonresidualproducts_kernel(tc, u, v, y, gm, gn, us, vs_byte
 
         def weigh_m(s):
             g = s // 8
+            if s % 2 == 0:
+                new("rm_woven%d" % (s // 2), [P, 2 * P, PACK], BF16, "rm_woven", 3)
             nc.vector.tensor_tensor(
-                out=new("rm_woven%d" % s, [P, P, PACK], BF16, "rm_woven", 4)[:],
+                out=T["rm_woven%d" % (s // 2)][:, P * (s % 2) : P * (s % 2 + 1), :],
                 in0=T["res%d" % s][:].rearrange("p t n -> p n t"),
                 in1=T["gm_neg"][:, g : g + 1, :].to_broadcast([P, P, PACK]),
                 op=MULT,
@@ -236,7 +296,23 @@ def tile_weightedpoissonresidualproducts_kernel(tc, u, v, y, gm, gn, us, vs_byte
             )
 
         def quant_rm(s):
-            quantize("rm%d" % s, slice(0, P), T["rm_woven%d" % s][:].rearrange("p n t -> p (n t)"))
+            cols = slice(P * (s % 2), P * (s % 2 + 1))
+            quantize("rm%d" % (s // 2), cols, T["rm_woven%d" % (s // 2)][:, cols, :].rearrange("p n t -> p (n t)"))
+
+        def quant_rm_pair(c):
+            quantize("rm%d" % c, slice(0, 2 * P), T["rm_woven%d" % c][:].rearrange("p n t -> p (n t)"))
+
+        def weave_us_piece(k):
+            dst = new("us_piece%d" % k, [P, K // 2, PACK], BF16, "us_piece", 1)
+            cols = slice((k % 2) * K // 2, (k % 2 + 1) * K // 2)
+            nc.gpsimd.tensor_scalar(
+                out=dst[:], in0=T["us_raw%d" % (k // 2)][:, :, cols].rearrange("p t c -> p c t"),
+                scalar1=1.0, scalar2=0.0, op0=MULT, op1=ADD,
+            )
+
+        def quant_us_piece(k):
+            cols = slice((k % 2) * K // 2, (k % 2 + 1) * K // 2)
+            quantize("us%d" % (k // 2), cols, T["us_piece%d" % k][:].rearrange("p c t -> p (c t)"))
 
         def gu_pass(g, t, h, tag):
             if h == 0:
@@ -246,7 +322,7 @@ def tile_weightedpoissonresidualproducts_kernel(tc, u, v, y, gm, gn, us, vs_byte
         def gv_pass(j, g, tag):
             if g == 0:
                 bank("gv%d" % j, tag, [P, K])
-            product(T["gv%d" % j][:], "rm%d" % (8 * g + j), slice(0, P), "us%d" % g, g == 0, g == 1)
+            product(T["gv%d" % j][:], "rm%d" % (4 * g + j // 2), slice(P * (j % 2), P * (j % 2 + 1)), "us%d" % g, g == 0, g == 1)
 
         def store(name, dst, engine):
             res = new(name + "_out", [P, K], F32, "result", 10)
@@ -265,68 +341,68 @@ def tile_weightedpoissonresidualproducts_kernel(tc, u, v, y, gm, gn, us, vs_byte
 
         BANKS = {"m": 4, "r": 4}
         constants()
-        load_u(0, 0); load_u(0, 1); load_v(0); load_vs_scale(); load_vs(0); load_gn(); load_v(1); load_y(0); load_gm()
-        load_v(2); load_v(3); load_vs(1); load_u(1, 0); load_u(1, 1); load_y(1); load_us(0); load_us(1); load_y(2); load_y(3)
-        negate_identity()
+        load_vs_scale(); load_gm(); load_gn()
+        load_vs(0); load_v_single(0); load_u(0, 0); load_u(0, 1); load_v_single(1); load_v(1); load_y(0); load_us(0); load_v(2); load_v(3)
+        load_u(1, 0); load_vs(1); load_u(1, 1); load_us(1); load_y(1); load_y(2); load_y(3)
+        negate_identity(); negate_gm()
+        for slot in range(4):
+            widen_vs(0, slot, "v")
+        turn_v_single(0, "m"); copy_v_single(0, "s")
         turn_k("u_raw00", "m"); copy_u(0, 0, "s")
-        turn_k("u_raw01", "m"); copy_u(0, 1, "s")
-        turn_k("v_raw0", "m"); copy_v(0, "s")
-        widen_vs(0, 0, "v")
-        quant_u(0, 0); widen_vs(0, 1, "v"); quant_u(0, 1); widen_vs(0, 2, "v")
-        quant_v(0)
-        spread_gn(0, "r"); spread_gn(1, "r")
-        turn_k("v_raw1", "m"); copy_gn(0); copy_v(1, "v")
-        theta(0, "m"); theta(1, "m")
-        open_residual(0, "r"); open_residual(1, "r")
-        rate(0); rate(1); copy_gn(1)
-        widen_vs(0, 3, "v")
-        quant_v(1)
-        weave("vs_wide0", 0, "v"); weave("vs_wide0", 1, "v")
-        negate_gm()
-        turn_k("v_raw2", "m"); close_residual(0); close_residual(1); copy_v(2, "s")
+        turn_k("u_raw01", "m")
+        weave("vs_wide0", 0, "v"); quant_v_single(0); weave("vs_wide0", 1, "v"); copy_u(0, 1, "v"); quant_u(0, 0); quant_u(0, 1)
+        turn_v_single(1, "m"); copy_v_single(1, "s")
+        spread_gn(0, "r"); spread_gn(1, "r"); copy_gn(0)
+        turn_k("v_raw1", "m")
+        theta_half(0, "m"); theta_half(1, "m"); rate_half(0); rate_half(1)
+        quant_v_single(1); copy_v(1, "v"); quant_woven("vs0", "vs_wide0"); quant_v(1)
+        theta(1, "m"); rate(1); open_residual(0, "r"); close_half(0); close_half(1)
+        copy_gn(1)
+        turn_k("v_raw2", "m"); copy_v(2, "s"); residual(1, "r")
+        weave_piece(0)
         theta(2, "m"); theta(3, "m"); rate(2); rate(3)
-        turn_k("v_raw3", "m"); copy_v(3, "s"); residual(2, "r"); residual(3, "r"); turn_k("u_raw10", "m"); copy_u(1, 0, "s")
-        weigh_m(0); weigh_n(0); quant_woven("vs0", "vs_wide0"); quant_rm(0); quant_v(2)
+        turn_k("v_raw3", "m"); copy_v(3, "s"); turn_k("u_raw10", "m"); copy_u(1, 0, "s"); residual(2, "r"); residual(3, "r")
+        widen_vs(1, 0, "s"); widen_vs(1, 1, "s")
+        turn_k("u_raw11", "m"); copy_u(1, 1, "s")
+        weigh_m(0); weigh_n(0); weigh_m(1); weigh_n(1); quant_v(2); quant_rm_pair(0); quant_piece(0); quant_v(3)
+        weave_piece(1)
         theta(4, "m"); theta(5, "m"); rate(4); rate(5)
-        weigh_m(1); weigh_n(1); quant_v(3); quant_rm(1); quant_u(1, 0)
-        turn_k("u_raw11", "m"); copy_u(1, 1, "s"); residual(4, "r"); residual(5, "r")
-        theta(6, "m"); theta(7, "m"); widen_vs(1, 0, "s"); widen_vs(1, 1, "s"); rate(6); rate(7)
-        weigh_m(2); weigh_n(2); quant_u(1, 1); quant_rm(2)
-        theta(8, "m"); theta(9, "m"); widen_vs(1, 2, "s"); widen_vs(1, 3, "s"); rate(8); rate(9)
-        weigh_n(3); weigh_m(3)
-        residual(6, "r"); residual(7, "r"); turn_rn(0, 0, "m"); copy_rn(0, 0, "s"); turn_rn(0, 1, "m"); copy_rn(0, 1, "s")
-        theta(10, "m"); theta(11, "m"); rate(10); rate(11)
-        weigh_m(4); quant_rm(3); weigh_n(4); quant_rm(4)
-        weigh_n(5); weave("vs_wide1", 0, "v"); weigh_n(6); weave("vs_wide1", 1, "v"); weigh_n(7); quant_rn(0, 0); quant_rn(0, 1); weigh_m(5)
-        weave("us_raw0", 0, "s", 4); weave("us_raw0", 1, "s", 4)
-        residual(8, "r"); turn_rn(1, 0, "m"); copy_rn(1, 0, "s"); turn_rn(1, 1, "m"); copy_rn(1, 1, "s")
-        weave("us_raw0", 2, "s", 4); weave("us_raw0", 3, "s", 4)
-        quant_woven("vs1", "vs_wide1"); quant_rm(5); weigh_m(6); weigh_m(7); quant_rn(1, 0); quant_rm(6); quant_rn(1, 1); quant_rm(7)
-        residual(9, "r"); residual(10, "r"); residual(11, "r")
-        weave("us_raw1", 0, "s", 4); weave("us_raw1", 1, "s", 4)
-        for t in (0, 1):
+        widen_vs(1, 2, "s"); widen_vs(1, 3, "s")
+        theta(6, "m"); theta(7, "m"); rate(6); rate(7)
+        weigh_n(2); weigh_n(3); weigh_m(2); weigh_m(3); quant_u(1, 0); quant_u(1, 1); quant_piece(1); quant_rm_pair(1)
+        residual(4, "r"); residual(5, "r"); turn_rn(0, 0, "m"); copy_rn(0, 0, "s"); turn_rn(0, 1, "m"); copy_rn(0, 1, "s")
+        weave_piece(2)
+        residual(6, "r"); residual(7, "r")
+        for s in range(8, 14):
+            theta(s, "m"); rate(s)
+        weigh_m(4); weigh_n(4); weigh_m(5); weigh_n(5); quant_rn(0, 0); quant_rn(0, 1); quant_piece(2); quant_rm_pair(2)
+        weave_piece(3)
+        residual(8, "r"); residual(9, "r")
+        weigh_n(6); weigh_n(7); weigh_m(6); weigh_m(7)
+        turn_rn(1, 0, "m"); copy_rn(1, 0, "s"); turn_rn(1, 1, "m"); copy_rn(1, 1, "s")
+        for s in range(14, 16):
+            theta(s, "m"); rate(s)
+        quant_piece(3); quant_rm_pair(3); quant_rn(1, 0); quant_rn(1, 1)
+        residual(10, "r"); residual(11, "r")
+        for t in range(4):
             gu_pass(0, t, 0, "m"); gu_pass(0, t, 1, "m"); store_gu(0, t, "s")
-        theta(12, "m"); theta(13, "m"); rate(12); rate(13)
-        for t in (2, 3):
-            gu_pass(0, t, 0, "m"); gu_pass(0, t, 1, "m"); store_gu(0, t, "s")
-        theta(14, "m"); theta(15, "m"); rate(14); rate(15)
-        weigh_m(8); weave("us_raw1", 1, "v", 2); weigh_n(8); quant_woven("us0", "us_raw0"); quant_rm(8); quant_woven("us1", "us_raw1")
-        weigh_m(9); weigh_n(9)
-        residual(12, "r")
-        weigh_m(10); quant_rm(9); weigh_n(10); quant_rm(10); weigh_n(11); weigh_m(11)
+        weigh_m(8); weigh_m(9); weigh_n(8); quant_rm_pair(4); weigh_n(9)
+        residual(12, "r"); residual(13, "r")
         for j in (0, 1):
             gv_pass(j, 0, "m"); gv_pass(j, 1, "m"); store_gv(j, "s")
-        residual(13, "r"); residual(14, "r"); turn_rn(2, 0, "m"); copy_rn(2, 0, "s"); turn_rn(2, 1, "m"); copy_rn(2, 1, "s"); residual(15, "r")
-        weigh_m(12); quant_rm(11); weigh_n(12); quant_rm(12)
-        for j in (2, 3, 4):
+        weigh_n(10); weigh_n(11); weigh_m(10); weigh_m(11)
+        turn_rn(2, 0, "m"); copy_rn(2, 0, "s"); residual(14, "r"); residual(15, "r"); turn_rn(2, 1, "m"); copy_rn(2, 1, "s")
+        weigh_n(12); quant_rm_pair(5); weigh_n(13); weigh_n(14); weigh_n(15)
+        for j in (2, 3):
             gv_pass(j, 0, "m"); gv_pass(j, 1, "m"); store_gv(j, "s")
-        weigh_n(13); weigh_n(14); weigh_n(15); quant_rn(2, 0); quant_rn(2, 1); weigh_m(13)
         turn_rn(3, 0, "m"); copy_rn(3, 0, "s"); turn_rn(3, 1, "m"); copy_rn(3, 1, "s")
-        gu_pass(1, 0, 0, "r"); gu_pass(1, 1, 0, "m")
-        weigh_m(14); quant_rm(13); quant_rn(3, 0); weigh_m(15); quant_rm(14); quant_rn(3, 1); quant_rm(15)
-        gv_pass(5, 0, "m"); gv_pass(5, 1, ""); store_gv(5, "s"); gu_pass(1, 0, 1, ""); gu_pass(1, 1, 1, ""); store_gu(1, 0, "s")
-        gv_pass(6, 0, "r"); gv_pass(6, 1, "")
-        store_gu(1, 1, "v"); store_gv(6, "s")
-        gu_pass(1, 2, 0, "m"); gu_pass(1, 2, 1, ""); store_gu(1, 2, "v")
-        gu_pass(1, 3, 0, "m"); gu_pass(1, 3, 1, ""); store_gu(1, 3, "s")
-        gv_pass(7, 0, "r"); gv_pass(7, 1, ""); store_gv(7, "v")
+        weigh_m(12); quant_rn(2, 0); quant_rm(12); weigh_m(13); quant_rn(2, 1); quant_rm(13); weigh_m(14); quant_rn(3, 0); quant_rn(3, 1); quant_rm(14); weigh_m(15)
+        for j in (4, 5):
+            gv_pass(j, 0, "r"); gv_pass(j, 1, ""); store_gv(j, "s")
+        quant_rm(15)
+        for t in range(2):
+            gu_pass(1, t, 0, "m"); gu_pass(1, t, 1, ""); store_gu(1, t, "s")
+        gv_pass(6, 0, "m"); gv_pass(6, 1, ""); store_gv(6, "v")
+        for t in range(2, 4):
+            gu_pass(1, t, 0, "mr"[t % 2]); gu_pass(1, t, 1, ""); store_gu(1, t, "sv"[t % 2])
+        gv_pass(7, 0, "r"); gv_pass(7, 1, ""); store_gv(7, "s")

@@ -267,13 +267,8 @@ def tile_weightedpoissonresidualproducts_kernel(tc, u, v, y, gm, gn, us, vs_byte
                 add_rate(s, t)
 
         def residual(s, tag):
-            b = bank("res%d" % s, tag, [P, PACK, P])
-            cols = slice(P * (s % 4), P * (s % 4 + 1))
-            for t in range(PACK + 1):
-                if t < PACK:
-                    nc.tensor.matmul(out=b[:, t, :], lhsT=T["neg_ident"][:], rhs=T["y%d" % (s // 4)][:, t, cols], start=(t == 0), stop=False)
-                if t > 0:
-                    add_rate(s, t - 1)
+            open_residual(s, tag)
+            close_residual(s)
 
         def weigh_m(s):
             g = s // 8

@@ -17,387 +17,448 @@ ADD = mybir.AluOpType.add
 EXP = mybir.ActivationFunctionType.Exp
 COPY = mybir.ActivationFunctionType.Copy
 
-ENG = mybir.EngineType
-PINNED = {ENG.PE, ENG.SP, ENG.Pool, ENG.DVE, ENG.Activation}
-
 P = 128
 PACK = 4
 PASS = P * PACK
-ROW_OF_SLOT = (0, 2, 1, 3)
-PIECE = 384
-WOVEN_BY_GPSIMD = (("us_raw0", "us0"), ("us_raw1", "us1"), ("vs_wide1", "vs1"))
+CHUNKS = N // P
+PAIRS = P // 2
+VS_ROW = (0, 2, 1, 3)
+
+BANKS_PER_TAG = 4
+RATE_BUFS = 6
+RM_BUFS = 5
+RESULT_BUFS = 10
+
+GPSIMD_WEAVES = (("us_raw0", "us0"), ("us_raw1", "us1"), ("vs_wide1", "vs1"))
+PIECE = len(GPSIMD_WEAVES) * K // 4
+
+
+def span(i, width, count=1):
+    return slice(i * width, (i + count) * width)
 
 
 def tile_weightedpoissonresidualproducts_kernel(tc, u, v, y, gm, gn, us, vs_bytes, vs_scale, out_0, out_1):
     nc = tc.nc
+    on_scalar = nc.scalar.copy
+    on_vector = nc.vector.tensor_copy
+
     with ExitStack() as ctx:
-        sb = ctx.enter_context(tc.tile_pool(name="sb", bufs=1))
-        ps = ctx.enter_context(tc.psum_pool(name="ps", bufs=1))
-        ctx.enter_context(tc.manual_schedule(engines=PINNED))
-        T = {}
+        sbuf = ctx.enter_context(tc.tile_pool(name="sbuf", bufs=1))
+        psum = ctx.enter_context(tc.psum_pool(name="psum", bufs=1))
+        ctx.enter_context(tc.manual_schedule())
+        tiles = {}
 
-        def new(key, shape, dtype, tag="", bufs=1):
-            T[key] = sb.tile(shape, dtype, name=key, tag=tag or key, bufs=bufs, align_bytes=256)
-            return T[key]
+        def new(name, shape, dtype, tag=None, bufs=1):
+            tiles[name] = sbuf.tile(shape, dtype, name=name, tag=tag or name, bufs=bufs, align_bytes=256)
+            return tiles[name]
 
-        def bank(key, tag, shape):
-            T[key] = ps.tile(shape, F32, name=key, tag=tag, bufs=BANKS[tag])
-            return T[key]
+        def bank(name, tag, shape):
+            tiles[name] = psum.tile(shape, F32, name=name, tag=tag, bufs=BANKS_PER_TAG)
+            return tiles[name]
 
-        def operand(key, width):
-            new(key + "_codes", [P, width], U32)
-            new(key + "_scales", [P, width], U8)
+        def operand(name, columns):
+            new(name + "_codes", [P, columns], U32)
+            new(name + "_scales", [P, columns], U8)
 
-        def quantize(key, cols, values):
-            nc.vector.quantize_mx(out=T[key + "_codes"][:, cols].bitcast(FP8X4), scales=T[key + "_scales"][:, cols], in_=values)
+        def quantize(name, cols, woven):
+            nc.vector.quantize_mx(
+                out=tiles[name + "_codes"][:, cols].bitcast(FP8X4), scales=tiles[name + "_scales"][:, cols], in_=woven
+            )
 
-        def product(out, lhs, cols, rhs, start, stop, moving=slice(0, PASS)):
+        def product(out, lhs, lhs_cols, rhs, rhs_cols, start, stop):
             nc.tensor.matmul_mx(
                 out=out,
-                lhsT=T[lhs + "_codes"][:, cols].bitcast(FP8X4),
-                lhsT_scale=T[lhs + "_scales"][:, cols],
-                rhs=T[rhs + "_codes"][:, moving].bitcast(FP8X4),
-                rhs_scale=T[rhs + "_scales"][:, moving],
+                lhsT=tiles[lhs + "_codes"][:, lhs_cols].bitcast(FP8X4),
+                lhsT_scale=tiles[lhs + "_scales"][:, lhs_cols],
+                rhs=tiles[rhs + "_codes"][:, rhs_cols].bitcast(FP8X4),
+                rhs_scale=tiles[rhs + "_scales"][:, rhs_cols],
                 start=start,
                 stop=stop,
             )
 
-        for i in range(2):
-            operand("u%d" % i, PASS)
-            operand("us%d" % i, K)
-            operand("vs%d" % i, K)
-        for i in range(4):
-            operand("v%d" % i, 2 * P)
-            operand("rn%d" % i, PASS)
-            new("rn_rows%d" % i, [P, PACK, 2, 2 * P], BF16)
-        for i in range(8):
-            operand("rm%d" % i, 2 * P)
-        new("gn_neg", [P, 8, 2, 64], BF16)
+        operand("v", N)
+        new("v_words", [P, 2 * N], F32)
+        for half in range(2):
+            operand("u%d" % half, PASS)
+            new("u%d_words" % half, [P, 2 * PASS], F32)
+            operand("us%d" % half, K)
+            operand("vs%d" % half, K)
+            operand("rm%d" % half, N)
+        for quarter in range(4):
+            operand("rn%d" % quarter, PASS)
+            new("rn%d_words" % quarter, [P, 2 * PASS], F32)
+            new("rn_rows%d" % quarter, [P, PACK, 2, 2 * P], BF16)
+        gn_neg = new("gn_neg", [P, CHUNKS, 2, PAIRS], BF16)
 
-        def constants():
-            ident = new("ident", [P, P], F32)
-            make_identity(nc, ident[:])
-            nc.vector.memset(new("gn_row", [P, N], BF16)[:], 0.0)
-            nc.vector.memset(new("minus_ones", [P, P], BF16)[:], -1.0)
+        def load(name, shape, dtype, src, queue=nc.sync):
+            queue.dma_start(out=new(name, shape, dtype)[:], in_=src)
 
-        def negate_identity():
-            nc.vector.tensor_scalar(out=new("neg_ident", [P, P], BF16)[:], in0=T["ident"][:], scalar1=-1.0, scalar2=None, op0=MULT)
+        def by_fours(x, half):
+            return x.rearrange("(a p t) c -> a p t c", p=P, t=PACK)[half]
 
         def load_u(g, a):
-            src = u.rearrange("(g p t) k -> g p t k", p=P, t=PACK)[g]
-            nc.sync.dma_start(out=new("u_raw%d%d" % (g, a), [P, 2, K], BF16)[:], in_=src[:, 2 * a : 2 * a + 2, :])
+            load("u_raw%d%d" % (g, a), [P, 2, K], BF16, by_fours(u, g)[:, span(a, 2), :])
 
-        def load_v(c):
-            nc.sync.dma_start(out=new("v_raw%d" % c, [P, 2, K], BF16)[:], in_=v.rearrange("(c p r) k -> c p r k", p=P, r=2)[c])
+        def load_v_chunk(j):
+            load("v_chunk%d" % j, [P, 1, K], BF16, v.rearrange("(j p o) k -> j p o k", p=P, o=1)[j])
 
-        def load_y(q):
-            src = y.rearrange("(g p t) n -> g p t n", p=P, t=PACK)[q // 2]
-            nc.sync.dma_start(out=new("y%d" % q, [P, PACK, PASS], BF16)[:], in_=src[:, :, PASS * (q % 2) : PASS * (q % 2 + 1)])
+        def load_v_pair(c):
+            load("v_pair%d" % c, [P, 2, K], BF16, v.rearrange("(c p r) k -> c p r k", p=P, r=2)[c])
+
+        def load_y(quarter):
+            load("y%d" % quarter, [P, PACK, PASS], BF16, by_fours(y, quarter // 2)[:, :, span(quarter % 2, PASS)])
 
         def load_us(g):
-            nc.sync.dma_start(out=new("us_raw%d" % g, [P, PACK, K], BF16)[:], in_=us.rearrange("(g p t) k -> g p t k", p=P, t=PACK)[g])
+            load("us_raw%d" % g, [P, PACK, K], BF16, by_fours(us, g))
 
         def load_vs(h):
-            nc.sync.dma_start(out=new("vs_raw%d" % h, [P, PACK, K], U8)[:], in_=vs_bytes.rearrange("(h p t) k -> h p t k", p=P, t=PACK)[h])
+            load("vs_raw%d" % h, [P, PACK, K], U8, by_fours(vs_bytes, h))
 
-        def load_gn():
-            nc.scalar.dma_start(out=T["gn_row"][0:1, :], in_=gn.rearrange("(o n) -> o n", o=1))
-
-        def load_gm():
-            nc.scalar.dma_start(out=new("gm_raw", [P, 2, PACK], BF16)[:], in_=gm.rearrange("(g p t) -> p g t", p=P, t=PACK))
-
-        def load_vs_scale():
-            nc.scalar.dma_start(out=new("vs_sc", [P, 2, PACK], F32)[:], in_=vs_scale.rearrange("(h p t) o -> p h (t o)", p=P, t=PACK))
-
-        def negate_gm():
-            nc.vector.tensor_scalar(out=new("gm_neg", [P, 2, PACK], F32)[:], in0=T["gm_raw"][:], scalar1=-1.0, scalar2=None, op0=MULT)
-
-        def spread_gn(h, tag):
-            b = bank("gn_ps%d" % h, tag, [P, PASS])
-            nc.tensor.matmul(out=b[:], lhsT=T["minus_ones"][:], rhs=T["gn_row"][:, PASS * h : PASS * (h + 1)], start=True, stop=True)
+        def spread_gn(h):
+            out = bank("gn_bank%d" % h, "residual", [P, PASS])
+            nc.tensor.matmul(out=out[:], lhsT=minus_ones[:], rhs=gn_row[:, span(h, PASS)], start=True, stop=True)
 
         def copy_gn(h):
-            nc.scalar.copy(out=T["gn_neg"][:, 4 * h : 4 * h + 4, :, :], in_=T["gn_ps%d" % h][:].rearrange("p (j i w) -> p j w i", j=4, w=2))
+            src = tiles["gn_bank%d" % h][:].rearrange("p (j i w) -> p j w i", i=PAIRS, w=2)
+            on_scalar(out=gn_neg[:, span(h, CHUNKS // 2), :, :], in_=src)
 
-        def turn_k(name, tag):
-            b = bank(name + "_ps", tag, [P, 2, 2, P])
-            for r in range(2):
-                words = T[name][:, r, :].bitcast(F32)
+        def turn(name, rows, words_of):
+            out = bank(name + "_bank", "rotating", [P, rows, 2, P])
+            for r in range(rows):
                 for w in range(2):
-                    nc.tensor.transpose(b[:, r, w, :], words[:, w : 2 * P : 2], T["ident"][:])
+                    nc.tensor.transpose(out[:, r, w, :], words_of(r, w), ident[:])
 
-        def turn_rn(q, a, tag):
-            b = bank("rn_t%d%d_ps" % (q, a), tag, [P, 2, 2, P])
-            for r in range(2):
-                for w in range(2):
-                    nc.tensor.transpose(b[:, r, w, :], T["rn_rows%d" % q][:, 2 * a + r, w, :].bitcast(F32), T["ident"][:])
+        def turn_k(name, rows=2):
+            turn(name, rows, lambda r, w: tiles[name][:, r, :].bitcast(F32)[:, w : 2 * P : 2])
 
-        def copy_words(name, order, engine):
-            dst = new(name + "_words", [P, PASS], F32, "words", 6)
-            src = T[name + "_ps"][:].rearrange("p r w m -> p " + order)
-            view = dst[:].rearrange("p (%s) -> p %s" % (order, order), r=2, w=2)
-            if engine == "s":
-                nc.scalar.copy(out=view, in_=src)
-            else:
-                nc.vector.tensor_copy(out=view, in_=src)
+        def turn_rn(quarter, a):
+            rows = tiles["rn_rows%d" % quarter]
+            turn("rn_turn%d%d" % (quarter, a), 2, lambda r, w: rows[:, 2 * a + r, w, :].bitcast(F32))
 
-        def copy_u(g, a, engine):
-            copy_words("u_raw%d%d" % (g, a), "r m w", engine)
-
-        def copy_v(c, engine):
-            copy_words("v_raw%d" % c, "m r w", engine)
-
-        def copy_rn(q, a, engine):
-            copy_words("rn_t%d%d" % (q, a), "r m w", engine)
-
-        def quant_u(g, a):
-            quantize("u%d" % g, slice(2 * P * a, 2 * P * (a + 1)), T["u_raw%d%d_words" % (g, a)][:].bitcast(BF16))
-
-        def quant_v(c):
-            quantize("v%d" % c, slice(0, 2 * P), T["v_raw%d_words" % c][:].bitcast(BF16))
-
-        def quant_rn(q, a):
-            quantize("rn%d" % q, slice(2 * P * a, 2 * P * (a + 1)), T["rn_t%d%d_words" % (q, a)][:].bitcast(BF16))
-
-        def widen_vs(h, slot, engine):
-            if slot == 0:
-                new("vs_wide%d" % h, [P, PACK, K], BF16)
-            t = ROW_OF_SLOT[slot]
-            codes = T["vs_raw%d" % h][:, t, :].bitcast(FP8)
-            scale = T["vs_sc"][:, h, t : t + 1]
-            if engine == "s":
-                nc.scalar.activation(out=T["vs_wide%d" % h][:, slot, :], in_=codes, func=COPY, scale=scale)
-            else:
-                nc.vector.tensor_scalar(out=T["vs_wide%d" % h][:, slot, :], in0=codes, scalar1=scale, scalar2=None, op0=MULT)
-
-        def weave(name, part, engine, parts=2):
-            if part == 0:
-                new(name + "_woven", [P, K, PACK], BF16)
-            cols = slice(part * K // parts, (part + 1) * K // parts)
-            if engine == "g":
-                nc.gpsimd.tensor_scalar(
-                    out=T[name + "_woven"][:, cols, :], in0=T[name][:, :, cols].rearrange("p t c -> p c t"),
-                    scalar1=1.0, scalar2=0.0, op0=MULT, op1=ADD,
-                )
-                return
-            dst = T[name + "_woven"][:, cols, :].rearrange("p (c i) t -> p c t i", i=4)
-            src = T[name][:, :, cols].rearrange("p t (c i) -> p c t i", i=4)
-            if engine == "s":
-                nc.scalar.copy(out=dst, in_=src)
-            else:
-                nc.vector.tensor_copy(out=dst, in_=src)
-
-        def quant_woven(key, name):
-            quantize(key, slice(0, K), T[name + "_woven"][:].rearrange("p c t -> p (c t)"))
-
-        def theta(s, tag):
-            j = s % 8
-            b = bank("theta%d" % s, tag, [P, PASS])
-            product(b[:], "v%d" % (j // 2), slice(P * (j % 2), P * (j % 2 + 1)), "u%d" % (s // 8), True, True)
-
-        def load_v_single(j):
-            nc.sync.dma_start(out=new("v_one%d" % j, [P, K], BF16)[:], in_=v[P * j : P * (j + 1), :])
-
-        def turn_v_single(j, tag):
-            b = bank("v_one%d_ps" % j, tag, [P, 2, P])
-            words = T["v_one%d" % j][:].bitcast(F32)
-            for w in range(2):
-                nc.tensor.transpose(b[:, w, :], words[:, w : 2 * P : 2], T["ident"][:])
-
-        def copy_v_single(j, engine):
-            dst = new("v_one%d_words" % j, [P, P, 2], F32)
-            src = T["v_one%d_ps" % j][:].rearrange("p w m -> p m w")
-            if engine == "s":
-                nc.scalar.copy(out=dst[:], in_=src)
-            else:
-                nc.vector.tensor_copy(out=dst[:], in_=src)
-
-        def quant_v_single(j):
-            quantize("v0", slice(P * j, P * (j + 1)), T["v_one%d_words" % j][:].rearrange("p m w -> p (m w)").bitcast(BF16))
-
-        def theta_half(a, tag):
-            b = bank("theta_half%d" % a, tag, [P, 2 * P])
-            product(b[:], "v0", slice(0, P), "u0", True, True, slice(2 * P * a, 2 * P * (a + 1)))
-
-        def rate_half(a):
-            if a == 0:
-                new("rate0", [P, PASS], F32, "rate", 10)
-            nc.scalar.activation(out=T["rate0"][:, 2 * P * a : 2 * P * (a + 1)], in_=T["theta_half%d" % a][:], func=EXP)
-
-        def close_half(a):
-            add_rate(0, 2 * a)
-            add_rate(0, 2 * a + 1)
-
-        def piece_parts(k):
-            parts = []
-            for i, (name, key) in enumerate(WOVEN_BY_GPSIMD):
-                lo, hi = max(PIECE * k, K * i), min(PIECE * (k + 1), K * (i + 1))
-                if lo < hi:
-                    parts.append((name, key, slice(lo - K * i, hi - K * i), slice(lo - PIECE * k, hi - PIECE * k)))
-            return parts
-
-        def weave_piece(k):
-            dst = new("piece%d" % k, [P, PIECE, PACK], BF16, "vs_wide0_woven", 1)
-            for name, key, cols, place in piece_parts(k):
-                nc.gpsimd.tensor_scalar(
-                    out=dst[:, place, :], in0=T[name][:, :, cols].rearrange("p t c -> p c t"),
-                    scalar1=1.0, scalar2=0.0, op0=MULT, op1=ADD,
-                )
-
-        def quant_piece(k):
-            for name, key, cols, place in piece_parts(k):
-                quantize(key, cols, T["piece%d" % k][:, place, :].rearrange("p c t -> p (c t)"))
-
-        def rate(s):
-            nc.scalar.activation(out=new("rate%d" % s, [P, PASS], F32, "rate", 10)[:], in_=T["theta%d" % s][:], func=EXP)
-
-        def open_residual(s, tag):
-            b = bank("res%d" % s, tag, [P, PACK, P])
-            cols = slice(P * (s % 4), P * (s % 4 + 1))
-            nc.tensor.matmul(out=b[:], lhsT=T["neg_ident"][:], rhs=T["y%d" % (s // 4)][:, :, cols], start=True, stop=False)
-
-        def add_rate(s, t):
-            nc.tensor.matmul(
-                out=T["res%d" % s][:, t, :], lhsT=T["rate%d" % s][:, P * t : P * (t + 1)], rhs=T["ident"][:],
-                is_transpose=True, start=False, stop=(t == PACK - 1),
+        def copy_words(name, rows, dst, first_col, order, copy):
+            words = tiles[dst + "_words"][:, 2 * first_col : 2 * (first_col + rows * P)]
+            copy(
+                out=words.rearrange("p (%s) -> p %s" % (order, order), r=rows, w=2),
+                in_=tiles[name + "_bank"][:].rearrange("p r w c -> p " + order),
             )
 
-        def close_residual(s):
-            for t in range(PACK):
-                add_rate(s, t)
+        def copy_u(g, a, copy=on_scalar):
+            copy_words("u_raw%d%d" % (g, a), 2, "u%d" % g, 2 * P * a, "r c w", copy)
 
-        def residual(s, tag):
-            open_residual(s, tag)
-            close_residual(s)
+        def copy_v_chunk(j):
+            copy_words("v_chunk%d" % j, 1, "v", P * j, "r c w", on_scalar)
+
+        def copy_v_pair(c):
+            copy_words("v_pair%d" % c, 2, "v", 2 * P * c, "c r w", on_scalar)
+
+        def turn_and_copy_rn(quarter):
+            for a in range(2):
+                turn_rn(quarter, a)
+                copy_words("rn_turn%d%d" % (quarter, a), 2, "rn%d" % quarter, 2 * P * a, "r c w", on_scalar)
+
+        def quantize_words(name, first_chunk, chunks):
+            words = tiles[name + "_words"][:, span(first_chunk, 2 * P, chunks)]
+            quantize(name, span(first_chunk, P, chunks), words.bitcast(BF16))
+
+        def widen_vs0():
+            wide = new("vs_wide0", [P, PACK, K], BF16)
+            for i, row in enumerate(VS_ROW):
+                nc.vector.tensor_scalar(
+                    out=wide[:, i, :], in0=tiles["vs_raw0"][:, row, :].bitcast(FP8),
+                    scalar1=tiles["vs_scale"][:, 0, row : row + 1], scalar2=None, op0=MULT,
+                )
+
+        def widen_vs1(i):
+            row = VS_ROW[i]
+            nc.scalar.activation(
+                out=tiles["vs_wide1"][:, i, :], in_=tiles["vs_raw1"][:, row, :].bitcast(FP8),
+                func=COPY, scale=tiles["vs_scale"][:, 1, row : row + 1],
+            )
+
+        def weave_vs0(a):
+            cols = span(a, K // 2)
+            on_vector(
+                out=tiles["vs_woven0"][:, cols, :].rearrange("p (c i) t -> p c t i", i=4),
+                in_=tiles["vs_wide0"][:, :, cols].rearrange("p t (c i) -> p c t i", i=4),
+            )
+
+        def piece_parts(piece):
+            parts = []
+            for i, (src, name) in enumerate(GPSIMD_WEAVES):
+                lo, hi = max(PIECE * piece, K * i), min(PIECE * (piece + 1), K * (i + 1))
+                if lo < hi:
+                    parts.append((src, name, slice(lo - K * i, hi - K * i), slice(lo - PIECE * piece, hi - PIECE * piece)))
+            return parts
+
+        def weave_piece(piece):
+            woven = new("piece%d" % piece, [P, PIECE, PACK], BF16, "woven")
+            for src, name, cols, place in piece_parts(piece):
+                nc.gpsimd.tensor_scalar(
+                    out=woven[:, place, :], in0=tiles[src][:, :, cols].rearrange("p t c -> p c t"),
+                    scalar1=1.0, scalar2=0.0, op0=MULT, op1=ADD,
+                )
+
+        def quantize_piece(piece):
+            for src, name, cols, place in piece_parts(piece):
+                quantize(name, cols, tiles["piece%d" % piece][:, place, :].rearrange("p c t -> p (c t)"))
+
+        def theta_and_rate(s):
+            out = bank("theta%d" % s, "rotating", [P, PASS])
+            product(out[:], "v", span(s % CHUNKS, P), "u%d" % (s // CHUNKS), span(0, PASS), True, True)
+            nc.scalar.activation(out=new("rate%d" % s, [P, PASS], F32, "rate", RATE_BUFS)[:], in_=out[:], func=EXP)
+
+        def first_theta_and_rate(a):
+            cols = span(a, PASS // 2)
+            out = bank("theta0_half%d" % a, "rotating", [P, PASS // 2])
+            product(out[:], "v", span(0, P), "u0", cols, True, True)
+            nc.scalar.activation(out=tiles["rate0"][:, cols], in_=out[:], func=EXP)
+
+        def add_y(s, first):
+            rhs = tiles["y%d" % (s // 4)][:, :, span(s % 4, P)]
+            nc.tensor.matmul(out=tiles["residual%d" % s][:], lhsT=neg_ident[:], rhs=rhs, start=first, stop=not first)
+
+        def add_rate(s, first):
+            for t in range(PACK):
+                nc.tensor.matmul(
+                    out=tiles["residual%d" % s][:, t, :], lhsT=tiles["rate%d" % s][:, span(t, P)], rhs=ident[:],
+                    is_transpose=True, start=first and t == 0, stop=not first and t == PACK - 1,
+                )
+
+        def open_residual(s):
+            bank("residual%d" % s, "residual", [P, PACK, P])
+            add_y(s, True)
+
+        def close_residual(s):
+            add_rate(s, False)
+
+        def residual_y_last(s):
+            bank("residual%d" % s, "residual", [P, PACK, P])
+            add_rate(s, True)
+            add_y(s, False)
 
         def weigh_m(s):
-            g = s // 8
             if s % 2 == 0:
-                new("rm_woven%d" % (s // 2), [P, 2 * P, PACK], BF16, "rm_woven", 3)
+                new("rm_woven%d" % (s // 2), [P, 2 * P, PACK], BF16, "rm_woven", RM_BUFS)
             nc.vector.tensor_tensor(
-                out=T["rm_woven%d" % (s // 2)][:, P * (s % 2) : P * (s % 2 + 1), :],
-                in0=T["res%d" % s][:].rearrange("p t n -> p n t"),
-                in1=T["gm_neg"][:, g : g + 1, :].to_broadcast([P, P, PACK]),
+                out=tiles["rm_woven%d" % (s // 2)][:, span(s % 2, P), :],
+                in0=tiles["residual%d" % s][:].rearrange("p t n -> p n t"),
+                in1=gm_neg[:, span(s // CHUNKS, 1), :].to_broadcast([P, P, PACK]),
                 op=MULT,
             )
 
         def weigh_n(s):
-            j = s % 8
             nc.vector.tensor_tensor(
-                out=T["rn_rows%d" % (s // 4)][:, :, :, 64 * (s % 4) : 64 * (s % 4 + 1)],
-                in0=T["res%d" % s][:].rearrange("p t (i w) -> p t w i", w=2),
-                in1=T["gn_neg"][:, j : j + 1, :, :].to_broadcast([P, PACK, 2, 64]),
+                out=tiles["rn_rows%d" % (s // 4)][:, :, :, span(s % 4, PAIRS)],
+                in0=tiles["residual%d" % s][:].rearrange("p t (i w) -> p t w i", w=2),
+                in1=gn_neg[:, span(s % CHUNKS, 1), :, :].to_broadcast([P, PACK, 2, PAIRS]),
                 op=MULT,
             )
 
-        def quant_rm(s):
-            cols = slice(P * (s % 2), P * (s % 2 + 1))
-            quantize("rm%d" % (s // 2), cols, T["rm_woven%d" % (s // 2)][:, cols, :].rearrange("p n t -> p (n t)"))
+        def quantize_rm(s, steps=2):
+            woven = tiles["rm_woven%d" % (s // 2)][:, span(s % 2, P, steps), :]
+            quantize("rm%d" % (s // CHUNKS), span(s % CHUNKS, P, steps), woven.rearrange("p n t -> p (n t)"))
 
-        def quant_rm_pair(c):
-            quantize("rm%d" % c, slice(0, 2 * P), T["rm_woven%d" % c][:].rearrange("p n t -> p (n t)"))
+        def result(name, tag, lhs, cols, rhs, dst, copy):
+            out = bank(name, tag, [P, K])
+            for i in range(2):
+                product(out[:], lhs[i], cols, "%s%d" % (rhs, i), span(0, K), i == 0, i == 1)
+            staged = new(name + "_staged", [P, K], F32, "result", RESULT_BUFS)
+            copy(out=staged[:], in_=out[:])
+            nc.sync.dma_start(out=dst, in_=staged[:])
 
-        def weave_us_piece(k):
-            dst = new("us_piece%d" % k, [P, K // 2, PACK], BF16, "us_piece", 1)
-            cols = slice((k % 2) * K // 2, (k % 2 + 1) * K // 2)
-            nc.gpsimd.tensor_scalar(
-                out=dst[:], in0=T["us_raw%d" % (k // 2)][:, :, cols].rearrange("p t c -> p c t"),
-                scalar1=1.0, scalar2=0.0, op0=MULT, op1=ADD,
-            )
+        def gu(g, t, tag="rotating", copy=on_scalar):
+            lhs = ("rn%d" % (2 * g), "rn%d" % (2 * g + 1))
+            result("gu%d%d" % (g, t), tag, lhs, span(t, P), "vs", by_fours(out_0, g)[:, t, :], copy)
 
-        def quant_us_piece(k):
-            cols = slice((k % 2) * K // 2, (k % 2 + 1) * K // 2)
-            quantize("us%d" % (k // 2), cols, T["us_piece%d" % k][:].rearrange("p c t -> p (c t)"))
-
-        def gu_pass(g, t, h, tag):
-            if h == 0:
-                bank("gu%d%d" % (g, t), tag, [P, K])
-            product(T["gu%d%d" % (g, t)][:], "rn%d" % (2 * g + h), slice(P * t, P * (t + 1)), "vs%d" % h, h == 0, h == 1)
-
-        def gv_pass(j, g, tag):
-            if g == 0:
-                bank("gv%d" % j, tag, [P, K])
-            product(T["gv%d" % j][:], "rm%d" % (4 * g + j // 2), slice(P * (j % 2), P * (j % 2 + 1)), "us%d" % g, g == 0, g == 1)
-
-        def store(name, dst, engine):
-            res = new(name + "_out", [P, K], F32, "result", 10)
-            if engine == "s":
-                nc.scalar.copy(out=res[:], in_=T[name][:])
-            else:
-                nc.vector.tensor_copy(out=res[:], in_=T[name][:])
-            nc.sync.dma_start(out=dst, in_=res[:])
-
-        def store_gu(g, t, engine):
-            store("gu%d%d" % (g, t), out_0.rearrange("(g p t) k -> g t p k", p=P, t=PACK)[g, t], engine)
-
-        def store_gv(j, engine):
-            store("gv%d" % j, out_1[P * j : P * (j + 1), :], engine)
+        def gv(j, tag="rotating", copy=on_scalar):
+            result("gv%d" % j, tag, ("rm0", "rm1"), span(j, P), "us", out_1[span(j, P), :], copy)
 
 
-        BANKS = {"m": 4, "r": 4}
-        constants()
-        load_vs_scale(); load_gm(); load_gn()
-        load_vs(0); load_v_single(0); load_u(0, 0); load_u(0, 1); load_v_single(1); load_v(1); load_y(0); load_us(0); load_v(2); load_v(3)
-        load_u(1, 0); load_vs(1); load_u(1, 1); load_us(1); load_y(1); load_y(2); load_y(3)
-        negate_identity(); negate_gm()
-        for slot in range(4):
-            widen_vs(0, slot, "v")
-        turn_v_single(0, "m"); copy_v_single(0, "s")
-        turn_k("u_raw00", "m"); copy_u(0, 0, "s")
-        turn_k("u_raw01", "m")
-        weave("vs_wide0", 0, "v"); quant_v_single(0); weave("vs_wide0", 1, "v"); copy_u(0, 1, "v"); quant_u(0, 0); quant_u(0, 1)
-        turn_v_single(1, "m"); copy_v_single(1, "s")
-        spread_gn(0, "r"); spread_gn(1, "r"); copy_gn(0)
-        turn_k("v_raw1", "m")
-        theta_half(0, "m"); theta_half(1, "m"); rate_half(0); rate_half(1)
-        quant_v_single(1); copy_v(1, "v"); quant_woven("vs0", "vs_wide0"); quant_v(1)
-        theta(1, "m"); rate(1); open_residual(0, "r"); close_half(0); close_half(1)
+        ident = new("ident", [P, P], F32)
+        make_identity(nc, ident[:])
+        gn_row = new("gn_row", [P, N], BF16)
+        nc.vector.memset(gn_row[:], 0.0)
+        minus_ones = new("minus_ones", [P, P], BF16)
+        nc.vector.memset(minus_ones[:], -1.0)
+
+        load("vs_scale", [P, 2, PACK], F32, vs_scale.rearrange("(h p t) o -> p h (t o)", p=P, t=PACK), nc.scalar)
+        load("gm_raw", [P, 2, PACK], BF16, gm.rearrange("(g p t) -> p g t", p=P, t=PACK), nc.scalar)
+        load("gn_raw", [1, N], BF16, gn.rearrange("(o n) -> o n", o=1))
+        load_vs(0)
+        load_v_chunk(0)
+        load_u(0, 0)
+        load_u(0, 1)
+        load_v_chunk(1)
+        load_v_pair(1)
+        load_y(0)
+        load_us(0)
+        load_v_pair(2)
+        load_vs(1)
+        load_v_pair(3)
+        load_u(1, 0)
+        load_y(1)
+        load_u(1, 1)
+        load_us(1)
+        load_y(2)
+        load_y(3)
+
+        neg_ident = new("neg_ident", [P, P], BF16)
+        nc.vector.tensor_scalar(out=neg_ident[:], in0=ident[:], scalar1=-1.0, scalar2=None, op0=MULT)
+        on_vector(out=gn_row[0:1, :], in_=tiles["gn_raw"][:])
+        widen_vs0()
+        spread_gn(0)
+        spread_gn(1)
+        copy_gn(0)
+        turn_k("v_chunk0", 1)
+        copy_v_chunk(0)
+        turn_k("u_raw00")
+        copy_u(0, 0)
         copy_gn(1)
-        turn_k("v_raw2", "m"); copy_v(2, "s"); residual(1, "r")
+        turn_k("u_raw01")
+        new("vs_woven0", [P, K, PACK], BF16, "woven")
+        weave_vs0(0)
+        quantize_words("v", 0, 1)
+        copy_u(0, 1, on_vector)
+        quantize_words("u0", 0, 2)
+        quantize_words("u0", 2, 2)
+        gm_neg = new("gm_neg", [P, 2, PACK], F32)
+        nc.vector.tensor_scalar(out=gm_neg[:], in0=tiles["gm_raw"][:], scalar1=-1.0, scalar2=None, op0=MULT)
+        turn_k("v_chunk1", 1)
+        copy_v_chunk(1)
+        turn_k("v_pair1")
+        copy_v_pair(1)
+        open_residual(0)
+        new("rate0", [P, PASS], F32, "rate", RATE_BUFS)
+        first_theta_and_rate(0)
+        first_theta_and_rate(1)
+        quantize_words("v", 1, 1)
+        weave_vs0(1)
+        quantize_words("v", 2, 2)
+        quantize("vs0", span(0, K), tiles["vs_woven0"][:].rearrange("p c t -> p (c t)"))
+        theta_and_rate(1)
+        open_residual(1)
+        close_residual(0)
+        turn_k("v_pair2")
+        copy_v_pair(2)
+        new("vs_wide1", [P, PACK, K], BF16)
+        widen_vs1(0)
+        open_residual(2)
+        close_residual(1)
+        turn_k("v_pair3")
+        copy_v_pair(3)
+        open_residual(3)
+
         weave_piece(0)
-        theta(2, "m"); theta(3, "m"); rate(2); rate(3)
-        turn_k("v_raw3", "m"); copy_v(3, "s"); turn_k("u_raw10", "m"); copy_u(1, 0, "s"); residual(2, "r"); residual(3, "r")
-        widen_vs(1, 0, "s"); widen_vs(1, 1, "s")
-        turn_k("u_raw11", "m"); copy_u(1, 1, "s")
-        weigh_m(0); weigh_n(0); weigh_m(1); weigh_n(1); quant_v(2); quant_rm_pair(0); quant_piece(0); quant_v(3)
+        theta_and_rate(2)
+        theta_and_rate(3)
+        widen_vs1(1)
+        for s in (0, 1):
+            weigh_m(s)
+            weigh_n(s)
+        turn_k("u_raw10")
+        copy_u(1, 0)
+        close_residual(2)
+        open_residual(4)
+        close_residual(3)
+        quantize_rm(0)
+        quantize_words("v", 4, 4)
+        quantize_piece(0)
+        turn_k("u_raw11")
+        copy_u(1, 1)
+        open_residual(5)
+
         weave_piece(1)
-        theta(4, "m"); theta(5, "m"); rate(4); rate(5)
-        widen_vs(1, 2, "s"); widen_vs(1, 3, "s")
-        theta(6, "m"); theta(7, "m"); rate(6); rate(7)
-        weigh_n(2); weigh_n(3); weigh_m(2); weigh_m(3); quant_u(1, 0); quant_u(1, 1); quant_piece(1); quant_rm_pair(1)
-        residual(4, "r"); residual(5, "r"); turn_rn(0, 0, "m"); copy_rn(0, 0, "s"); turn_rn(0, 1, "m"); copy_rn(0, 1, "s")
+        for s in range(4, 8):
+            theta_and_rate(s)
+        widen_vs1(2)
+        widen_vs1(3)
+        for weigh in (weigh_n, weigh_m):
+            weigh(2)
+            weigh(3)
+        quantize_words("u1", 0, 4)
+        quantize_piece(1)
+        open_residual(6)
+        close_residual(4)
+        close_residual(5)
+        turn_and_copy_rn(0)
+
         weave_piece(2)
-        residual(6, "r"); residual(7, "r")
-        for s in range(8, 14):
-            theta(s, "m"); rate(s)
-        weigh_m(4); weigh_n(4); weigh_m(5); weigh_n(5); quant_rn(0, 0); quant_rn(0, 1); quant_piece(2); quant_rm_pair(2)
+        open_residual(7)
+        close_residual(6)
+        close_residual(7)
+        for s in (4, 5):
+            weigh_m(s)
+            weigh_n(s)
+        quantize_rm(2)
+        quantize_piece(2)
+        open_residual(8)
+        for s in range(8, 13):
+            theta_and_rate(s)
+
         weave_piece(3)
-        residual(8, "r"); residual(9, "r")
-        weigh_n(6); weigh_n(7); weigh_m(6); weigh_m(7)
-        turn_rn(1, 0, "m"); copy_rn(1, 0, "s"); turn_rn(1, 1, "m"); copy_rn(1, 1, "s")
-        for s in range(14, 16):
-            theta(s, "m"); rate(s)
-        quant_piece(3); quant_rm_pair(3); quant_rn(1, 0); quant_rn(1, 1)
-        residual(10, "r"); residual(11, "r")
-        for t in range(4):
-            gu_pass(0, t, 0, "m"); gu_pass(0, t, 1, "m"); store_gu(0, t, "s")
-        weigh_m(8); weigh_m(9); weigh_n(8); quant_rm_pair(4); weigh_n(9)
-        residual(12, "r"); residual(13, "r")
-        for j in (0, 1):
-            gv_pass(j, 0, "m"); gv_pass(j, 1, "m"); store_gv(j, "s")
-        weigh_n(10); weigh_n(11); weigh_m(10); weigh_m(11)
-        turn_rn(2, 0, "m"); copy_rn(2, 0, "s"); residual(14, "r"); residual(15, "r"); turn_rn(2, 1, "m"); copy_rn(2, 1, "s")
-        weigh_n(12); quant_rm_pair(5); weigh_n(13); weigh_n(14); weigh_n(15)
-        for j in (2, 3):
-            gv_pass(j, 0, "m"); gv_pass(j, 1, "m"); store_gv(j, "s")
-        turn_rn(3, 0, "m"); copy_rn(3, 0, "s"); turn_rn(3, 1, "m"); copy_rn(3, 1, "s")
-        weigh_m(12); quant_rn(2, 0); quant_rm(12); weigh_m(13); quant_rn(2, 1); quant_rm(13); weigh_m(14); quant_rn(3, 0); quant_rn(3, 1); quant_rm(14); weigh_m(15)
-        for j in (4, 5):
-            gv_pass(j, 0, "r"); gv_pass(j, 1, ""); store_gv(j, "s")
-        quant_rm(15)
-        for t in range(2):
-            gu_pass(1, t, 0, "m"); gu_pass(1, t, 1, ""); store_gu(1, t, "s")
-        gv_pass(6, 0, "m"); gv_pass(6, 1, ""); store_gv(6, "v")
-        for t in range(2, 4):
-            gu_pass(1, t, 0, "mr"[t % 2]); gu_pass(1, t, 1, ""); store_gu(1, t, "sv"[t % 2])
-        gv_pass(7, 0, "r"); gv_pass(7, 1, ""); store_gv(7, "s")
+        open_residual(9)
+        close_residual(8)
+        close_residual(9)
+        for weigh in (weigh_n, weigh_m):
+            weigh(6)
+            weigh(7)
+        turn_and_copy_rn(1)
+        quantize_piece(3)
+        quantize_words("rn0", 0, 4)
+        quantize_words("rn1", 0, 4)
+        open_residual(10)
+        close_residual(10)
+        residual_y_last(11)
+
+        for s in range(13, 16):
+            theta_and_rate(s)
+        for t in range(PACK):
+            gu(0, t)
+        weigh_m(8)
+        weigh_m(9)
+        weigh_n(8)
+        quantize_rm(8)
+        weigh_n(9)
+        quantize_rm(4)
+
+        open_residual(12)
+        close_residual(12)
+        residual_y_last(13)
+        gv(0)
+        gv(1)
+        for s in (10, 11):
+            weigh_n(s)
+            weigh_m(s)
+        quantize_rm(6)
+        open_residual(14)
+        close_residual(14)
+        turn_and_copy_rn(2)
+        residual_y_last(15)
+
+        weigh_n(12)
+        quantize_rm(10)
+        for s in (13, 14, 15):
+            weigh_n(s)
+        gv(2)
+        gv(3)
+        turn_and_copy_rn(3)
+        weigh_m(12)
+        quantize_words("rn2", 0, 4)
+        quantize_rm(12, 1)
+        weigh_m(13)
+        quantize_words("rn3", 0, 2)
+        quantize_rm(13, 1)
+        quantize_words("rn3", 2, 2)
+        weigh_m(14)
+        weigh_m(15)
+        quantize_rm(14, 1)
+
+        gv(4, "residual")
+        gv(5, "residual")
+        quantize_rm(15, 1)
+        gu(1, 0)
+        gu(1, 1)
+        gv(6, "rotating", on_vector)
+        gu(1, 2)
+        gu(1, 3, "residual", on_vector)
+        gv(7, "residual")

from contextlib import ExitStack

import concourse.mybir as mybir
from concourse.masks import make_identity

M, N, K = 1024, 1024, 512
FLOPS = 3 * 2 * M * N * K

F32 = mybir.dt.float32
BF16 = mybir.dt.bfloat16
U32 = mybir.dt.uint32
U8 = mybir.dt.uint8
FP8 = mybir.dt.float8_e4m3fn
FP8X4 = mybir.dt.float8_e4m3fn_x4
MULT = mybir.AluOpType.mult
ADD = mybir.AluOpType.add
EXP = mybir.ActivationFunctionType.Exp
COPY = mybir.ActivationFunctionType.Copy

P = 128
PACK = 4
PASS = P * PACK
CHUNKS = N // P
PAIRS = P // 2
VS_ROW = (0, 2, 1, 3)

BANKS_PER_TAG = 4
RATE_BUFS = 6
RM_BUFS = 5
RESULT_BUFS = 10

GPSIMD_WEAVES = (("us_raw0", "us0"), ("us_raw1", "us1"), ("vs_wide1", "vs1"))
PIECE = len(GPSIMD_WEAVES) * K // 4


def span(i, width, count=1):
    return slice(i * width, (i + count) * width)


def tile_weightedpoissonresidualproducts_kernel(tc, u, v, y, gm, gn, us, vs_bytes, vs_scale, out_0, out_1):
    nc = tc.nc
    on_scalar = nc.scalar.copy
    on_vector = nc.vector.tensor_copy

    with ExitStack() as ctx:
        sbuf = ctx.enter_context(tc.tile_pool(name="sbuf", bufs=1))
        psum = ctx.enter_context(tc.psum_pool(name="psum", bufs=1))
        ctx.enter_context(tc.manual_schedule())
        tiles = {}

        def new(name, shape, dtype, tag=None, bufs=1):
            tiles[name] = sbuf.tile(shape, dtype, name=name, tag=tag or name, bufs=bufs, align_bytes=256)
            return tiles[name]

        def bank(name, tag, shape):
            tiles[name] = psum.tile(shape, F32, name=name, tag=tag, bufs=BANKS_PER_TAG)
            return tiles[name]

        def operand(name, columns):
            new(name + "_codes", [P, columns], U32)
            new(name + "_scales", [P, columns], U8)

        def quantize(name, cols, woven):
            nc.vector.quantize_mx(
                out=tiles[name + "_codes"][:, cols].bitcast(FP8X4), scales=tiles[name + "_scales"][:, cols], in_=woven
            )

        def product(out, lhs, lhs_cols, rhs, rhs_cols, start, stop):
            nc.tensor.matmul_mx(
                out=out,
                lhsT=tiles[lhs + "_codes"][:, lhs_cols].bitcast(FP8X4),
                lhsT_scale=tiles[lhs + "_scales"][:, lhs_cols],
                rhs=tiles[rhs + "_codes"][:, rhs_cols].bitcast(FP8X4),
                rhs_scale=tiles[rhs + "_scales"][:, rhs_cols],
                start=start,
                stop=stop,
            )

        operand("v", N)
        new("v_words", [P, 2 * N], F32)
        for half in range(2):
            operand("u%d" % half, PASS)
            new("u%d_words" % half, [P, 2 * PASS], F32)
            operand("us%d" % half, K)
            operand("vs%d" % half, K)
            operand("rm%d" % half, N)
        for quarter in range(4):
            operand("rn%d" % quarter, PASS)
            new("rn%d_words" % quarter, [P, 2 * PASS], F32)
            new("rn_rows%d" % quarter, [P, PACK, 2, 2 * P], BF16)
        gn_neg = new("gn_neg", [P, CHUNKS, 2, PAIRS], BF16)

        def load(name, shape, dtype, src, queue=nc.sync):
            queue.dma_start(out=new(name, shape, dtype)[:], in_=src)

        def by_fours(x, half):
            return x.rearrange("(a p t) c -> a p t c", p=P, t=PACK)[half]

        def load_u(g, a):
            load("u_raw%d%d" % (g, a), [P, 2, K], BF16, by_fours(u, g)[:, span(a, 2), :])

        def load_v_chunk(j):
            load("v_chunk%d" % j, [P, 1, K], BF16, v.rearrange("(j p o) k -> j p o k", p=P, o=1)[j])

        def load_v_pair(c):
            load("v_pair%d" % c, [P, 2, K], BF16, v.rearrange("(c p r) k -> c p r k", p=P, r=2)[c])

        def load_y(quarter):
            load("y%d" % quarter, [P, PACK, PASS], BF16, by_fours(y, quarter // 2)[:, :, span(quarter % 2, PASS)])

        def load_us(g):
            load("us_raw%d" % g, [P, PACK, K], BF16, by_fours(us, g))

        def load_vs(h):
            load("vs_raw%d" % h, [P, PACK, K], U8, by_fours(vs_bytes, h))

        def spread_gn(h):
            out = bank("gn_bank%d" % h, "residual", [P, PASS])
            nc.tensor.matmul(out=out[:], lhsT=minus_ones[:], rhs=gn_row[:, span(h, PASS)], start=True, stop=True)

        def copy_gn(h):
            src = tiles["gn_bank%d" % h][:].rearrange("p (j i w) -> p j w i", i=PAIRS, w=2)
            on_scalar(out=gn_neg[:, span(h, CHUNKS // 2), :, :], in_=src)

        def turn(name, rows, words_of):
            out = bank(name + "_bank", "rotating", [P, rows, 2, P])
            for r in range(rows):
                for w in range(2):
                    nc.tensor.transpose(out[:, r, w, :], words_of(r, w), ident[:])

        def turn_k(name, rows=2):
            turn(name, rows, lambda r, w: tiles[name][:, r, :].bitcast(F32)[:, w : 2 * P : 2])

        def turn_rn(quarter, a):
            rows = tiles["rn_rows%d" % quarter]
            turn("rn_turn%d%d" % (quarter, a), 2, lambda r, w: rows[:, 2 * a + r, w, :].bitcast(F32))

        def copy_words(name, rows, dst, first_col, order, copy):
            words = tiles[dst + "_words"][:, 2 * first_col : 2 * (first_col + rows * P)]
            copy(
                out=words.rearrange("p (%s) -> p %s" % (order, order), r=rows, w=2),
                in_=tiles[name + "_bank"][:].rearrange("p r w c -> p " + order),
            )

        def copy_u(g, a, copy=on_scalar):
            copy_words("u_raw%d%d" % (g, a), 2, "u%d" % g, 2 * P * a, "r c w", copy)

        def copy_v_chunk(j):
            copy_words("v_chunk%d" % j, 1, "v", P * j, "r c w", on_scalar)

        def copy_v_pair(c):
            copy_words("v_pair%d" % c, 2, "v", 2 * P * c, "c r w", on_scalar)

        def turn_and_copy_rn(quarter):
            for a in range(2):
                turn_rn(quarter, a)
                copy_words("rn_turn%d%d" % (quarter, a), 2, "rn%d" % quarter, 2 * P * a, "r c w", on_scalar)

        def quantize_words(name, first_chunk, chunks):
            words = tiles[name + "_words"][:, span(first_chunk, 2 * P, chunks)]
            quantize(name, span(first_chunk, P, chunks), words.bitcast(BF16))

        def widen_vs0():
            wide = new("vs_wide0", [P, PACK, K], BF16)
            for i, row in enumerate(VS_ROW):
                nc.vector.tensor_scalar(
                    out=wide[:, i, :], in0=tiles["vs_raw0"][:, row, :].bitcast(FP8),
                    scalar1=tiles["vs_scale"][:, 0, row : row + 1], scalar2=None, op0=MULT,
                )

        def widen_vs1(i):
            row = VS_ROW[i]
            nc.scalar.activation(
                out=tiles["vs_wide1"][:, i, :], in_=tiles["vs_raw1"][:, row, :].bitcast(FP8),
                func=COPY, scale=tiles["vs_scale"][:, 1, row : row + 1],
            )

        def weave_vs0(a):
            cols = span(a, K // 2)
            on_vector(
                out=tiles["vs_woven0"][:, cols, :].rearrange("p (c i) t -> p c t i", i=4),
                in_=tiles["vs_wide0"][:, :, cols].rearrange("p t (c i) -> p c t i", i=4),
            )

        def piece_parts(piece):
            parts = []
            for i, (src, name) in enumerate(GPSIMD_WEAVES):
                lo, hi = max(PIECE * piece, K * i), min(PIECE * (piece + 1), K * (i + 1))
                if lo < hi:
                    parts.append((src, name, slice(lo - K * i, hi - K * i), slice(lo - PIECE * piece, hi - PIECE * piece)))
            return parts

        def weave_piece(piece):
            woven = new("piece%d" % piece, [P, PIECE, PACK], BF16, "woven")
            for src, name, cols, place in piece_parts(piece):
                nc.gpsimd.tensor_scalar(
                    out=woven[:, place, :], in0=tiles[src][:, :, cols].rearrange("p t c -> p c t"),
                    scalar1=1.0, scalar2=0.0, op0=MULT, op1=ADD,
                )

        def quantize_piece(piece):
            for src, name, cols, place in piece_parts(piece):
                quantize(name, cols, tiles["piece%d" % piece][:, place, :].rearrange("p c t -> p (c t)"))

        def theta_and_rate(s):
            out = bank("theta%d" % s, "rotating", [P, PASS])
            product(out[:], "v", span(s % CHUNKS, P), "u%d" % (s // CHUNKS), span(0, PASS), True, True)
            nc.scalar.activation(out=new("rate%d" % s, [P, PASS], F32, "rate", RATE_BUFS)[:], in_=out[:], func=EXP)

        def first_theta_and_rate(a):
            cols = span(a, PASS // 2)
            out = bank("theta0_half%d" % a, "rotating", [P, PASS // 2])
            product(out[:], "v", span(0, P), "u0", cols, True, True)
            nc.scalar.activation(out=tiles["rate0"][:, cols], in_=out[:], func=EXP)

        def add_y(s, first):
            rhs = tiles["y%d" % (s // 4)][:, :, span(s % 4, P)]
            nc.tensor.matmul(out=tiles["residual%d" % s][:], lhsT=neg_ident[:], rhs=rhs, start=first, stop=not first)

        def add_rate(s, first):
            for t in range(PACK):
                nc.tensor.matmul(
                    out=tiles["residual%d" % s][:, t, :], lhsT=tiles["rate%d" % s][:, span(t, P)], rhs=ident[:],
                    is_transpose=True, start=first and t == 0, stop=not first and t == PACK - 1,
                )

        def open_residual(s):
            bank("residual%d" % s, "residual", [P, PACK, P])
            add_y(s, True)

        def close_residual(s):
            add_rate(s, False)

        def residual_y_last(s):
            bank("residual%d" % s, "residual", [P, PACK, P])
            add_rate(s, True)
            add_y(s, False)

        def weigh_m(s):
            if s % 2 == 0:
                new("rm_woven%d" % (s // 2), [P, 2 * P, PACK], BF16, "rm_woven", RM_BUFS)
            nc.vector.tensor_tensor(
                out=tiles["rm_woven%d" % (s // 2)][:, span(s % 2, P), :],
                in0=tiles["residual%d" % s][:].rearrange("p t n -> p n t"),
                in1=gm_neg[:, span(s // CHUNKS, 1), :].to_broadcast([P, P, PACK]),
                op=MULT,
            )

        def weigh_n(s):
            nc.vector.tensor_tensor(
                out=tiles["rn_rows%d" % (s // 4)][:, :, :, span(s % 4, PAIRS)],
                in0=tiles["residual%d" % s][:].rearrange("p t (i w) -> p t w i", w=2),
                in1=gn_neg[:, span(s % CHUNKS, 1), :, :].to_broadcast([P, PACK, 2, PAIRS]),
                op=MULT,
            )

        def quantize_rm(s, steps=2):
            woven = tiles["rm_woven%d" % (s // 2)][:, span(s % 2, P, steps), :]
            quantize("rm%d" % (s // CHUNKS), span(s % CHUNKS, P, steps), woven.rearrange("p n t -> p (n t)"))

        def result(name, tag, lhs, cols, rhs, dst, copy):
            out = bank(name, tag, [P, K])
            for i in range(2):
                product(out[:], lhs[i], cols, "%s%d" % (rhs, i), span(0, K), i == 0, i == 1)
            staged = new(name + "_staged", [P, K], F32, "result", RESULT_BUFS)
            copy(out=staged[:], in_=out[:])
            nc.sync.dma_start(out=dst, in_=staged[:])

        def gu(g, t, tag="rotating", copy=on_scalar):
            lhs = ("rn%d" % (2 * g), "rn%d" % (2 * g + 1))
            result("gu%d%d" % (g, t), tag, lhs, span(t, P), "vs", by_fours(out_0, g)[:, t, :], copy)

        def gv(j, tag="rotating", copy=on_scalar):
            result("gv%d" % j, tag, ("rm0", "rm1"), span(j, P), "us", out_1[span(j, P), :], copy)


        ident = new("ident", [P, P], F32)
        make_identity(nc, ident[:])
        gn_row = new("gn_row", [P, N], BF16)
        nc.vector.memset(gn_row[:], 0.0)
        minus_ones = new("minus_ones", [P, P], BF16)
        nc.vector.memset(minus_ones[:], -1.0)

        load("vs_scale", [P, 2, PACK], F32, vs_scale.rearrange("(h p t) o -> p h (t o)", p=P, t=PACK), nc.scalar)
        load("gm_raw", [P, 2, PACK], BF16, gm.rearrange("(g p t) -> p g t", p=P, t=PACK), nc.scalar)
        load("gn_raw", [1, N], BF16, gn.rearrange("(o n) -> o n", o=1))
        load_vs(0)
        load_v_chunk(0)
        load_u(0, 0)
        load_u(0, 1)
        load_v_chunk(1)
        load_v_pair(1)
        load_y(0)
        load_us(0)
        load_v_pair(2)
        load_vs(1)
        load_v_pair(3)
        load_u(1, 0)
        load_y(1)
        load_u(1, 1)
        load_us(1)
        load_y(2)
        load_y(3)

        neg_ident = new("neg_ident", [P, P], BF16)
        nc.vector.tensor_scalar(out=neg_ident[:], in0=ident[:], scalar1=-1.0, scalar2=None, op0=MULT)
        on_vector(out=gn_row[0:1, :], in_=tiles["gn_raw"][:])
        widen_vs0()
        spread_gn(0)
        spread_gn(1)
        copy_gn(0)
        turn_k("v_chunk0", 1)
        copy_v_chunk(0)
        turn_k("u_raw00")
        copy_u(0, 0)
        copy_gn(1)
        turn_k("u_raw01")
        new("vs_woven0", [P, K, PACK], BF16, "woven")
        weave_vs0(0)
        quantize_words("v", 0, 1)
        copy_u(0, 1, on_vector)
        quantize_words("u0", 0, 2)
        quantize_words("u0", 2, 2)
        gm_neg = new("gm_neg", [P, 2, PACK], F32)
        nc.vector.tensor_scalar(out=gm_neg[:], in0=tiles["gm_raw"][:], scalar1=-1.0, scalar2=None, op0=MULT)
        turn_k("v_chunk1", 1)
        copy_v_chunk(1)
        turn_k("v_pair1")
        copy_v_pair(1)
        open_residual(0)
        new("rate0", [P, PASS], F32, "rate", RATE_BUFS)
        first_theta_and_rate(0)
        first_theta_and_rate(1)
        quantize_words("v", 1, 1)
        weave_vs0(1)
        quantize_words("v", 2, 2)
        quantize("vs0", span(0, K), tiles["vs_woven0"][:].rearrange("p c t -> p (c t)"))
        theta_and_rate(1)
        open_residual(1)
        close_residual(0)
        turn_k("v_pair2")
        copy_v_pair(2)
        new("vs_wide1", [P, PACK, K], BF16)
        widen_vs1(0)
        open_residual(2)
        close_residual(1)
        turn_k("v_pair3")
        copy_v_pair(3)
        open_residual(3)

        weave_piece(0)
        theta_and_rate(2)
        theta_and_rate(3)
        widen_vs1(1)
        for s in (0, 1):
            weigh_m(s)
            weigh_n(s)
        turn_k("u_raw10")
        copy_u(1, 0)
        close_residual(2)
        open_residual(4)
        close_residual(3)
        quantize_rm(0)
        quantize_words("v", 4, 4)
        quantize_piece(0)
        turn_k("u_raw11")
        copy_u(1, 1)
        open_residual(5)

        weave_piece(1)
        for s in range(4, 8):
            theta_and_rate(s)
        widen_vs1(2)
        widen_vs1(3)
        for weigh in (weigh_n, weigh_m):
            weigh(2)
            weigh(3)
        quantize_words("u1", 0, 4)
        quantize_piece(1)
        open_residual(6)
        close_residual(4)
        close_residual(5)
        turn_and_copy_rn(0)

        weave_piece(2)
        open_residual(7)
        close_residual(6)
        close_residual(7)
        for s in (4, 5):
            weigh_m(s)
            weigh_n(s)
        quantize_rm(2)
        quantize_piece(2)
        open_residual(8)
        for s in range(8, 13):
            theta_and_rate(s)

        weave_piece(3)
        open_residual(9)
        close_residual(8)
        close_residual(9)
        for weigh in (weigh_n, weigh_m):
            weigh(6)
            weigh(7)
        turn_and_copy_rn(1)
        quantize_piece(3)
        quantize_words("rn0", 0, 4)
        quantize_words("rn1", 0, 4)
        open_residual(10)
        close_residual(10)
        residual_y_last(11)

        for s in range(13, 16):
            theta_and_rate(s)
        for t in range(PACK):
            gu(0, t)
        weigh_m(8)
        weigh_m(9)
        weigh_n(8)
        quantize_rm(8)
        weigh_n(9)
        quantize_rm(4)

        open_residual(12)
        close_residual(12)
        residual_y_last(13)
        gv(0)
        gv(1)
        for s in (10, 11):
            weigh_n(s)
            weigh_m(s)
        quantize_rm(6)
        open_residual(14)
        close_residual(14)
        turn_and_copy_rn(2)
        residual_y_last(15)

        weigh_n(12)
        quantize_rm(10)
        for s in (13, 14, 15):
            weigh_n(s)
        gv(2)
        gv(3)
        turn_and_copy_rn(3)
        weigh_m(12)
        quantize_words("rn2", 0, 4)
        quantize_rm(12, 1)
        weigh_m(13)
        quantize_words("rn3", 0, 2)
        quantize_rm(13, 1)
        quantize_words("rn3", 2, 2)
        weigh_m(14)
        weigh_m(15)
        quantize_rm(14, 1)

        gv(4, "residual")
        gv(5, "residual")
        quantize_rm(15, 1)
        gu(1, 0)
        gu(1, 1)
        gv(6, "rotating", on_vector)
        gu(1, 2)
        gu(1, 3, "residual", on_vector)
        gv(7, "residual")
